import numpy as np, ml_dtypes
CORES = [23,119,17,113]
N = 4
import mx_ref
BF = ml_dtypes.bfloat16
def pick(q, e):
    c = np.concatenate([q[0].reshape(128, -1, 4), np.zeros((128, 1, 4), np.uint8)], axis=1); s = np.concatenate([q[1], np.ones((16, 1), np.uint8)], axis=1)
    return (np.ascontiguousarray(c[:, e].reshape(128, -1)), np.ascontiguousarray(s[:, e]))
def join(*qs):
    return (np.concatenate([q[0] for q in qs], axis=1), np.concatenate([q[1] for q in qs], axis=1))
def put(q, e, v):
    c, s = q[0].reshape(128, -1, 4).copy(), q[1].copy(); c[:, e] = v[0].reshape(128, -1, 4); s[:, e] = v[1]
    return (c.reshape(128, -1), s)
def pk(c, s):
    return (np.ascontiguousarray(c), mx_ref.live(s))
def emit(q):
    return q[0], q[1]
def cut(t, i, w=512):
    return t[:, w * i:w * i + w]
def tile(rs):
    return np.stack(rs, axis=2).reshape(128, -1).astype(BF)
def f(rng, *shape):
    return mx_ref.flush((rng.standard_normal(shape, dtype=np.float32) * np.exp2(rng.integers(-2, 3, shape[:-1] + (1,)))).astype(BF))
def wide(rng, *shape, cols=0):
    v = rng.standard_normal(shape, dtype=np.float32) * np.exp2(rng.integers(-12, 13, shape)).astype(np.float32)
    if cols: v *= np.repeat(np.exp2(rng.integers(-cols, cols + 1, shape[:-2] + (1, shape[-1] // 4))) * (rng.random(shape[:-2] + (1, shape[-1] // 4)) > 0.0625), 4, axis=-1).astype(np.float32)
    return mx_ref.flush(v.astype(BF))
T, L, CAPP = 256, 2, 64
def game(x, u, w):
    S = [mx_ref.quantize(np.ascontiguousarray(x[r])) for r in range(N)]
    qu = [mx_ref.quantize(np.ascontiguousarray(u[r])) for r in range(N)]
    at, ks, made = np.arange(N * T).reshape(N, T), np.zeros((N, 1, L), np.float32), []
    for b in range(L):
        want = [np.flatnonzero(mx_ref.matmul(qu[r], S[r])[b] + np.float32(0) < 0) for r in range(N)]
        new, now = [], at.copy()
        for r in range(N):
            p = r ^ (1 << b)
            k = min(len(want[r]), len(want[p]), CAPP)
            to, of = want[r][:k], want[p][:k]
            c = pick(S[p], np.concatenate([of, np.full(CAPP - k, -1)]))
            t = tile([np.float32(0.0625) * mx_ref.matmul(mx_ref.quantize(np.ascontiguousarray(cut(w[r], 4 * b + i))), c) for i in range(4)])
            made.append(t)
            new.append(put(S[r], to, pick(mx_ref.quantize(t), np.arange(k))))
            now[r, to] = at[p, of]
            ks[r, 0, b] = k
        S, at = new, now
    return S, at, ks, made
def fit(t, low, high):
    a = np.abs(t.astype(np.float32))
    return bool((np.isfinite(a) & ((a == 0) | (a >= low) & (a <= high))).all())
def blocks(t):
    return np.abs(t.astype(np.float32)).reshape(16, 8, -1, 4).max(axis=(1, 3))
def plain(rng):
    u = np.array(f(rng, N, 128, 512))
    u[:, :, 4 * L:] = 0
    a = np.exp2(rng.integers(-2, 3, (N, 128, 1, 1)))
    x, lean = rng.standard_normal((N, 128, T, 4)), 2.5 * rng.random((N, L)) - 1
    for b in range(L):
        h = a * u[:, :, None, 4 * b:4 * b + 4].astype(np.float64)
        x += lean[:, b, None, None, None] * h * np.sum(h * h, axis=(1, 2, 3), keepdims=True) ** -0.5
    x = mx_ref.flush((a * x).reshape(N, 128, 4 * T).astype(np.float32).astype(BF))
    return {"x": x, "u": u, "w": f(rng, N, 128, 2048 * L), "v": f(rng, N, 128, 512)}
def aim(x, u, wish):
    x = x.reshape(N, 128, T, 4).astype(np.float32)
    for r in range(N):
        s = mx_ref.matmul(mx_ref.quantize(np.ascontiguousarray(u[r])), mx_ref.quantize(np.ascontiguousarray(x[r].reshape(128, 4 * T).astype(BF))))[0]
        x[r][:, s == 0] = u[r][:, None, :4].astype(np.float32)
        x[r][:, (s < 0) != wish[r]] *= -1
    return (x + np.float32(0)).reshape(N, 128, 4 * T).astype(BF)
def some(rng, n):
    return np.stack([rng.permutation(T) < n[r] for r in range(N)])
def setup_inputs(rng):
    return plain(rng)
def setup_inputs_many(rng):
    d = plain(rng)
    n = rng.integers(CAPP + 1, T + 1, N)
    j = 2 * int(rng.integers(0, N // 2))
    n[j:j + 2] = CAPP
    d["x"] = aim(d["x"], d["u"], some(rng, n))
    return d
def setup_inputs_none(rng):
    d = plain(rng)
    wish = some(rng, rng.integers(T // 4, T + 1, N))
    i, j = 2 * rng.permutation(N // 2)[:2] + rng.integers(0, 2, 2)
    wish[i] = False
    wish[i ^ 1] = True
    wish[j] = np.arange(T) == T - 1
    d["u"][int(rng.integers(0, N)), :, 4:8] = 0
    d["x"] = aim(d["x"], d["u"], wish)
    return d
def setup_inputs_zero(rng):
    d = plain(rng)
    d["u"][:, 64:, :4] = 0
    x = np.array(d["x"]).reshape(N, 128, T, 4)
    for r in range(N):
        e = rng.permutation(T)
        x[r][:, e[:T // 8]] = 0
        x[r][:64, e[T // 8:3 * T // 8]] = 0
    d["x"] = x.reshape(N, 128, 4 * T)
    return d
def setup_inputs_turn(rng):
    d = plain(rng)
    d["x"] = aim(d["x"], d["u"], some(rng, np.full(N, T // 2)))
    m, e = np.zeros((128, L, 4, 128, 4), np.float32), np.arange(128)
    for b in range(L):
        for i in range(4): m[e, b, i, e, i] = -16
    d["w"] = mx_ref.flush((m.reshape(128, 2048 * L) + d["w"].astype(np.float32) * np.float32(2.0 ** -6)).astype(BF))
    return d
def setup_inputs_spread(rng):
    d = plain(rng)
    u = np.array(wide(rng, N, 128, 512))
    u[:, :, 4 * L:] = 0
    return {**d, "x": wide(rng, N, 128, 4 * T, cols=6), "u": u, "v": wide(rng, N, 128, 512)}
def check_inputs(d):
    b = []
    for k in ("x", "u", "w", "v"):
        if not fit(d[k], 2.0 ** -30, 2.0 ** 30): b.append("a value of " + k)
    if (d["u"][:, :, 4 * L:].astype(np.float32) != 0).any(): b.append("u has numbers behind its first L columns")
    if not b:
        try:
            made = game(d["x"], d["u"], d["w"])[3]
            good, even = all(fit(t, 2.0 ** -60, 2.0 ** 60) for t in made), all(fit(blocks(t), 2.0 ** -30, 2.0 ** 30) for t in made)
        except Exception: good = even = False
        if not good: b.append("a number that an expert gives")
        if not even: b.append("the largest number of a block that an expert gives")
    return b
def reference(x, u, w, v):
    S, at, ks, made = game(x, u, w)
    oc, osc = np.zeros((N, 128, 4 * T), np.uint8), np.zeros((N, 16, T), np.uint8)
    y = np.zeros((N, 128, T), np.float32)
    for r in range(N):
        oc[r], osc[r] = emit(S[r])
        y[r] = mx_ref.matmul(mx_ref.quantize(np.ascontiguousarray(v[r])), S[r])
    return {"oc": oc, "osc": osc, "ids": at.reshape(N, 1, T).astype(np.float32), "ks": ks, "y": y}

@@ -1,0 +1,359 @@
+from concourse.bass import DstId, RemoteDMATransfer
+from concourse.mybir import dt, AluOpType as A, ActivationFunctionType as AF
+
+F8, BF = "float8_e4m3fn_x4", "bfloat16"
+
+
+def _sb(n, t="float32"):
+    return ("sbuf", [128, n], t)
+
+
+SCRATCH = {
+    "cna": _sb(1), "cnb": _sb(1, BF), "cnta": _sb(1), "cntb": _sb(1, BF), "cnt1": _sb(1, BF),
+    "lin": _sb(4, "uint16"), "lin2": _sb(4, "uint16"), "pof": _sb(4, "uint16"),
+    "lin1": _sb(4, "uint16"), "offd": _sb(16, "uint16"), "pidx": _sb(2, "int32"), "pand": _sb(2, "int32"), "pand2": _sb(2, "int32"),
+}
+for _n, _k in dict(ub=8, xt=1024, wt=4096, vt=512, ut0=512, ut1=512, zt=512, ones=128, h0=512, h1=512, w0=288, w1=352, wn=64,
+                   sig=256, siga=128).items():
+    SCRATCH[_n] = _sb(_k, BF)
+for _n, _k in dict(qu0=128, qu1=128, qw=1024, qv=128, hold0=384, hold1=384, fin=256, snd0=64, snd1=64, z=256).items():
+    SCRATCH[_n + "c"], SCRATCH[_n + "s"] = _sb(_k, F8), _sb(_k, "uint8")
+for _n, _k in dict(pq=2, p31=2, r16=16, r32=16, jw=16, bias=2, lo=2, hi=2, ini=2, alt=20, acnt=1, th=2, ksb=2, row=256, pid=336,
+                   ptmp=64, idw0=384, idw1=384, idf=256, yrow=336, yn=64).items():
+    SCRATCH[_n] = _sb(_k)
+for _b in "01":
+    for _n, _k in dict(f=272, junk=256, clip=256, sums=256, wb=256, e=256, dup=256, dtr=256).items():
+        SCRATCH[_n + _b] = _sb(_k, BF)
+    for _n, _k in dict(acc=2, lf=4, gap=20, sel=20, mov=20, res=20).items():
+        SCRATCH[_n + _b] = _sb(_k)
+    SCRATCH["off" + _b], SCRATCH["offm" + _b] = _sb(4, "uint16"), _sb(20, "uint16")
+for _b in range(8):
+    SCRATCH["ps%d" % _b] = ("psum", [128, 512], "float32")
+
+REMOTE = ["rcnta", "rcntb", "rcod0", "rscl0", "rlst", "rpof", "rcnt1", "rlst1", "rcod1", "rscl1", "lall", "lcnt", "go"]
+POOL = 80
+SEMAPHORES = REMOTE + ["s%d" % _i for _i in range(POOL)]
+Z = (0, 128)
+NEW = (0, 64)
+
+
+def rank_program(g, core, T, topo):
+    rank = T.rank_of(core)
+    if rank is None:
+        return
+    cores = T.cores
+    mate0, mate1, far = rank ^ 1, rank ^ 2, rank ^ 3
+    V, S, P, Y = g.vector, g.scalar, g.tensor, g.sync
+    ops, local = [], {"lall": 0, "lcnt": 0}
+
+    def op(name, queue, fn, *deps, dma=False):
+        ops.append((name, queue, fn, deps, dma))
+
+    def eng(a, b):
+        return len(topo.engines(cores[a], cores[b]))
+    arrive = {"A.lst": ("rlst", eng(mate0, rank) + eng(far, rank)), "A.pof": ("rpof", eng(mate1, rank)),
+              "A.lst1": ("rlst1", eng(mate1, rank)), "A.cnt1": ("rcnt1", eng(mate1, rank)),
+              "A.cnta": ("rcnta", eng(mate0, rank)), "A.cntb": ("rcntb", eng(mate0, rank)),
+              "E.go": ("go", 1), "L.cnt": ("lcnt", eng(rank, mate0))}
+    for b, m in ((0, mate0), (1, mate1)):
+        for kind in ("cod", "scl"):
+            arrive["A.%s%d" % (kind, b)] = ("r%s%d" % (kind, b), eng(m, rank))
+
+    def send(name, to, dst, src, sem, *deps, lsem="lall"):
+        rid, pid, _ = topo.addr(cores[to])
+        local[lsem] += eng(rank, to)
+        op(name, g, lambda: g.remote_dma(out_ap=dst, in_ap=src, remote_sem=T.sem[sem], local_sem=T.sem[lsem], pid=pid,
+                                         routing_id=rid, dma_engine_mask=topo.mask(core, cores[to])), *deps)
+
+    def u8(v):
+        return v.bitcast(dt.uint8)
+
+    def u32(v):
+        return v.bitcast(dt.uint32)
+
+    def mm(name, bank, n, wc, ws, xc, xs, *deps):
+        op(name, P, lambda: P.matmul_mx(T["ps%d" % bank][:, 0:n], wc, ws, xc, xs, True, True), *deps)
+
+    def ts(name, out, in0, s1, s2, o0, o1, *deps):
+        if o1 is None:
+            op(name, V, lambda: V.tensor_scalar(out, in0, s1, None, o0), *deps)
+        else:
+            op(name, V, lambda: V.tensor_scalar(out, in0, s1, s2, o0, o1), *deps)
+
+    def tt(name, out, a, b, o, *deps):
+        op(name, V, lambda: V.tensor_tensor(out, a, b, o), *deps)
+
+    def tc(name, out, in_, *deps):
+        op(name, V, lambda: V.tensor_copy(out, in_), *deps)
+
+    def scan(name, out, a, b, init, o0, o1, *deps):
+        op(name, V, lambda: V.tensor_tensor_scan(out, a, b, init, o0, o1), *deps)
+
+    def act(name, out, in_, fn, *deps, **kw):
+        op(name, S, lambda: S.activation(out, in_, fn, **kw), *deps)
+
+    def quant(name, qc, qs, t, *deps):
+        op(name, V, lambda: V.quantize_mx(qc, qs, t), *deps)
+
+    def move(name, q, out, in_, *deps):
+        op(name, q, lambda: q.dma_start(out, in_), *deps, dma=True)
+
+    def iota(name, out, pattern, base, cm, flag):
+        if flag:
+            op(name, g, lambda: g.iota(out, pattern, base, cm, allow_small_or_imprecise_dtypes=True))
+        else:
+            op(name, g, lambda: g.iota(out, pattern, base, cm))
+
+    move("ld.u", S, T.ub[:, 0:8], T.u[:, 0:8])
+    move("ld.xA", Y, T.xt[:, 0:512], T.x[:, 0:512])
+    move("ld.xB", Y, T.xt[:, 512:1024], T.x[:, 512:1024])
+    move("ld.w0", Y, T.wt[:, 0:2048], T.w[:, 0:2048])
+
+    iota("i.p", T.pidx[:], [[0, 2]], 0, 1, False)
+    iota("i.r16", T.r16[:], [[16, 16]], 0, 0, True)
+    iota("i.r32", T.r32[:], [[32, 8], [0, 2]], 0, 0, True)
+    op("m.ones", V, lambda: V.memset(T.ones[:], 1.0))
+    op("m.zt", V, lambda: V.memset(T.zt[:], 0.0))
+    ts("c.and", T.pand[:], T.pidx[:], 15, None, A.bitwise_and, None, "i.p")
+    ts("c.and2", T.pand2[:], T.pidx[:], 31, None, A.bitwise_and, None, "i.p")
+    tc("c.pq", T.pq[:], T.pand[:], "c.and")
+    tc("c.p31", T.p31[:], T.pand2[:], "c.and2")
+    ts("c.jw", T.jw[:], T.r16[:], T.pq[:, 0:1], None, A.add, None, "c.pq", "i.r16")
+    ts("c.offd", T.offd[:], T.r32[:], T.p31[:, 0:1], None, A.add, None, "c.p31", "i.r32")
+    quant("q.z", T.zc[:, 64:192], T.zs[:, 64:192], T.zt[:], "m.zt")
+    for b in range(2):
+        act("m.h%d" % b, T["h%d" % b][:, 256:512], T.zt[:, 0:256], AF.Copy, "m.zt")
+    for b, w, k in ((0, T.w0, 288), (1, T.w1, 280)):
+        act("m.a%d" % b, w[:, 0:16], T.zt[:, 0:16], AF.Copy, "m.zt")
+        act("m.b%d" % b, w[:, 272:k], T.zt[:, 0:k - 272], AF.Copy, "m.zt")
+
+    for t in range(3):
+        ts("u0.%d" % t, T.ut0[:, t:512:4], T.ones[:, 0:128], T.ub[:, t:t + 1], None, A.mult, None, "ld.u", "m.ones")
+    act("u0.3", T.ut0[:, 3:512:4], T.zt[:, 0:128], AF.Identity, "ld.u", "m.zt", bias=T.ub[:, 3:4])
+    act("c.bias", T.bias[:], T.jw[:, 2:4], AF.Copy, "c.jw", scale=128.0, bias=64.0)
+    act("c.lo", T.lo[:], T.jw[:, 0:2], AF.Copy, "c.jw", scale=128.0)
+    act("c.hi", T.hi[:], T.jw[:, 0:2], AF.Copy, "c.jw", scale=128.0, bias=128.0)
+    act("c.ini", T.ini[:], T.jw[:, 0:2], AF.Copy, "c.jw", scale=16384.0, bias=16384.0)
+    for t in range(4):
+        act("u1.%d" % t, T.ut1[:, t:512:4], T.zt[:, 0:128], AF.Identity, "ld.u", "m.zt", bias=T.ub[:, 4 + t:5 + t])
+    quant("q.u0", T.qu0c[:], T.qu0s[:], T.ut0[:], "u0.0", "u0.1", "u0.2", "u0.3")
+
+    X = ("q.xA", "q.xB")
+    quant("q.xA", T.hold0c[:, 128:256], T.hold0s[:, 128:256], T.xt[:, 0:512], "ld.xA")
+    mm("t.sA", 0, 128, T.qu0c[:], T.qu0s[:], T.hold0c[:, 128:256], T.hold0s[:, 128:256], "q.u0", "q.xA")
+    act("sg.A", T.siga[:], T.ps0[:, 0:128], AF.Sign, "t.sA", scale=-1.0)
+    act("w.A", T.w0[:, 16:144], T.siga[:], AF.Relu, "sg.A", scale=64.0, accum_out=T.cna[:, 0:1])
+    quant("q.xB", T.hold0c[:, 256:384], T.hold0s[:, 256:384], T.xt[:, 512:1024], "ld.xB")
+    mm("t.sB", 1, 128, T.qu0c[:], T.qu0s[:], T.hold0c[:, 256:384], T.hold0s[:, 256:384], "q.u0", "q.xB")
+    scan("f.A", T.f0[:, 0:128], T.w0[:, 16:144], T.w0[:, 15:143], 0.0, A.add, A.add, "w.A", "m.a0")
+    act("wb.A", T.wb0[:, 0:128], T.w0[:, 15:143], AF.Copy, "w.A", "m.a0", scale=1.015625)
+    ts("w.B", T.w0[:, 144:272], T.ps1[:, 0:128], 0.0, 64.0, A.is_lt, A.mult, "t.sB")
+    scan("f.0", T.f0[:, 128:257], T.w0[:, 144:273], T.w0[:, 143:272], T.f0[:, 127:128], A.add, A.add, "w.B", "f.A", "m.b0")
+
+    def lists(b):
+        f, acc, cl, su, off, junk = (T[k % b] for k in ("f%d", "acc%d", "clip%d", "sums%d", "off%d", "junk%d"))
+        n = "f.%d" % b
+        for m in range(2):
+            act("ps%d.%d" % (m, b), junk[:, 128 * m:128 * m + 112], f[:, 33:256:2], AF.Sign, n, "c.bias", scale=-1.0,
+                bias=T.bias[:, m:m + 1], accum_out=acc[:, m:m + 1])
+        for m in range(2):
+            ts("pm%d.%d" % (m, b), cl[:, 128 * m:128 * m + 128], f[:, 1:256:2], T.lo[:, m:m + 1], T.hi[:, m:m + 1], A.max, A.min,
+               n, "c.lo", "c.hi")
+        if not b:
+            ts("n.B", T.cnb[:], f[:, 256:257], T.cna[:, 0:1], T.cna[:, 0:1], A.subtract, A.subtract, n, "w.A")
+        for m in range(2):
+            scan("pc%d.%d" % (m, b), su[:, 128 * m:128 * m + 128], T.ones[:, 0:128], cl[:, 128 * m:128 * m + 128],
+                 T.ini[:, m:m + 1], A.mult, A.subtract, "pm%d.%d" % (m, b), "c.ini")
+        p = 0 if b else 128
+        act("wb.B%d" % b, T["wb%d" % b][:, p:256], T["w%d" % b][:, 15 + p:271], AF.Copy, n, scale=1.015625)
+        ts("os.%d" % b, off[:, 2:4], acc[:, 0:2], 111.0, 144.0, A.min, A.add, "ps0.%d" % b, "ps1.%d" % b)
+        ts("ov.%d" % b, off[:, 0:2], su[:, 127:256:128], 0.015625, 255.0, A.mult, A.min, "pc0.%d" % b, "pc1.%d" % b)
+
+    def pick(name, oc, os, ic, is_, off, deps):
+        op(name + "c", V, lambda: V.tensor_copy(u32(oc), u32(ic).indirect(off)), *deps)
+        op(name + "s", S, lambda: S.activation(os, is_.indirect(off), AF.Copy), *deps)
+
+    def merge(b, i, p, q, *deps):
+        oc, os, c = (T.finc, T.fins, 0) if b else (T.hold1c, T.hold1s, 128)
+        pick("mg%d%d" % (b, i), oc[:, c + p:c + q], os[:, c + p:c + q], T["hold%dc" % b][:, 0:384], T["hold%ds" % b][:, 0:384],
+             T["offm%d" % b][:, 4 + p // 16:4 + q // 16], ("om.%d" % b, "q.n%d" % b) + deps)
+
+    def escan(b):
+        scan("e.%d" % b, T["e%d" % b][:], T["wb%d" % b][:], T["w%d" % b][:, 16:272], 64.0, A.add, A.subtract, "wb.B%d" % b,
+             "f.%d" % b, *(() if b else ("wb.A",)))
+        tc("lf.%d" % b, T["lf%d" % b][:], T["off%d" % b][:, 0:4], "ov.%d" % b, "os.%d" % b)
+        act("dup.%d" % b, T["dup%d" % b][:], T["e%d" % b][:, 0:256].indirect(T.offd[:, 0:16]), AF.Copy, "e.%d" % b, "c.offd")
+
+    def gap4(b):
+        tt("g4.%d" % b, T["gap%d" % b][:, 0:4], T["lf%d" % b][:], T.alt[:, 0:4], A.subtract, "lf.%d" % b, "c.alt0")
+
+    def laid(b):
+        op("tr.%d" % b, V, lambda: V.transpose(T["dtr%d" % b][:], T["dup%d" % b][:]), "dup.%d" % b)
+
+    def gap16(b):
+        tt("g16.%d" % b, T["gap%d" % b][:, 4:20], T["dtr%d" % b][:, 0:256:16], T.alt[:, 4:20], A.subtract, "tr.%d" % b, "c.alt1")
+
+    def settle(b, part):
+        own = T["f%d" % b][:, 256:257]
+        if part == 0:
+            if b:
+                ts("th.1", T.th[:, 1:2], T.cnt1[:, 0:1], own, 8192.0, A.min, A.min, "A.cnt1", "f.1")
+            else:
+                ts("nn.0", T.acnt[:], T.cntb[:, 0:1], T.cnta[:, 0:1], T.cnta[:, 0:1], A.add, A.add, "A.cnta", "A.cntb")
+        if part == 1 and not b:
+            ts("th.0", T.th[:, 0:1], T.acnt[:], own, 8192.0, A.min, A.min, "nn.0", "f.0")
+        if part == 2:
+            ts("s4.%d" % b, T["sel%d" % b][:, 0:4], T.jw[:, 0:4], 128.0, T.th[:, b:b + 1], A.mult, A.is_lt, "th.%d" % b, "c.jw")
+            ts("s16.%d" % b, T["sel%d" % b][:, 4:20], T["dtr%d" % b][:, 0:256:16], 128.0, T.th[:, b:b + 1], A.mult, A.is_lt,
+               "th.%d" % b, "tr.%d" % b)
+        if part == 3:
+            tt("mv.%d" % b, T["mov%d" % b][:], T["sel%d" % b][:], T["gap%d" % b][:], A.mult, "s4.%d" % b, "s16.%d" % b,
+               "g4.%d" % b, "g16.%d" % b)
+        if part == 4:
+            tt("rs.%d" % b, T["res%d" % b][:], T["mov%d" % b][:], T.alt[:], A.add, "mv.%d" % b, "c.alt0", "c.alt1")
+        if part == 5:
+            tc("om.%d" % b, T["offm%d" % b][:], T["res%d" % b][:], "rs.%d" % b)
+
+    def expert(b, i):
+        a, c = 512 * b + 128 * i, 2048 * b + 512 * i
+        quant("q.w%d%d" % (i, b), T.qwc[:, a:a + 128], T.qws[:, a:a + 128], T.wt[:, c:c + 512], "ld.w%d" % b)
+
+    def fresh(b, between=None):
+        h, hold, z = T["h%d" % b], "hold%d" % b, Z[b]
+        for i in range(4):
+            a = 512 * b + 128 * i
+            mm("R%d.%d" % (i, b), 4 + i, 128, T.qwc[:, a:a + 128], T.qws[:, a:a + 128], T.zc[:, z:z + 128], T.zs[:, z:z + 128],
+               "q.w%d%d" % (i, b), "q.z", "A.cod%d" % b, "A.scl%d" % b, *(("K%d.0" % i,) if b else ()))
+        for i in range(4):
+            r = T["ps%d" % (4 + i)][:, NEW[b]:NEW[b] + 64]
+            if i == 3:
+                ts("K%d.%d" % (i, b), h[:, i:256:4], r, 0.0625, None, A.mult, None, "R%d.%d" % (i, b))
+            else:
+                act("K%d.%d" % (i, b), h[:, i:256:4], r, AF.Copy, "R%d.%d" % (i, b), scale=0.0625)
+                if i == 0 and between is not None:
+                    between()
+        quant("q.n%d" % b, T[hold + "c"][:, 0:128], T[hold + "s"][:, 0:128], h[:],
+              *["K%d.%d" % (i, b) for i in range(4)], "m.h%d" % b)
+
+    send("g.cnta", mate0, T.cnta[:, 0:1], T.cna[:, 0:1], "rcnta", "w.A", lsem="lcnt")
+    lists(0)
+    send("g.cntb", mate0, T.cntb[:, 0:1], T.cnb[:, 0:1], "rcntb", "n.B")
+    pick("pk0", T.snd0c[:], T.snd0s[:], T.hold0c[:, 128:384], T.hold0s[:, 128:384], T.off0[:, 0:4], ("ov.0", "os.0") + X)
+    send("g.cod0", mate0, u8(T.zc[:, 0:64]), u8(T.snd0c[:, 0:64]), "rcod0", "pk0c")
+    send("g.scl0", mate0, T.zs[:, 0:64], T.snd0s[:, 0:64], "rscl0", "pk0s")
+    to = [topo.addr(cores[r]) for r in (mate0, far)]
+    local["lall"] += eng(rank, mate0)
+    op("g.lst", g, lambda: g.remote_dma_fused([RemoteDMATransfer(
+        dst_ids=[DstId(rid=a[0], pnc=a[1]) for a in to],
+        dma_engine_mask=topo.mask(core, cores[mate0]) & topo.mask(core, cores[far]),
+        remote_sem=T.sem["rlst"], srcs=[T.off0[:, 0:4]], dsts=[T.lin[:], T.lin2[:]])], local_sem=T.sem["lall"]), "ov.0", "os.0")
+    op("g.go", g, lambda: g.sem_inc(T.sem["go"], 1))
+    move("ld.v", Y, T.vt[:], T.v[:], "E.go", "L.cnt")
+    move("ld.w1", Y, T.wt[:, 2048:4096], T.w[:, 2048:4096])
+    iota("i.row", T.row[:], [[1, 256]], 0, 0, True)
+    iota("i.idw0", T.idw0[:], [[1, 384]], 256 * rank - 128, 0, True)
+
+    act("c.alt0", T.alt[:, 0:4], T.jw[:, 0:4], AF.Copy, "c.jw", bias=264.0)
+    act("c.alt1", T.alt[:, 4:20], T.jw[:], AF.Copy, "c.jw", bias=128.0)
+    escan(0)
+    quant("q.u1", T.qu1c[:], T.qu1s[:], T.ut1[:], "u1.0", "u1.1", "u1.2", "u1.3")
+    mm("t.s1", 2, 256, T.qu1c[:], T.qu1s[:], T.hold0c[:, 128:384], T.hold0s[:, 128:384], "q.u1", *X)
+    act("sg.1", T.sig[:], T.ps2[:, 0:256], AF.Sign, "t.s1", scale=-1.0)
+    act("w.1x", T.w1[:, 16:272], T.sig[:], AF.Relu, "sg.1", scale=64.0)
+    expert(0, 0)
+    gap4(0)
+    expert(0, 1)
+    expert(0, 2)
+    expert(0, 3)
+    laid(0)
+    settle(0, 0)
+    gap16(0)
+    for part in range(1, 6):
+        settle(0, part)
+    send("g.pof", mate1, T.pof[:], T.offm0[:, 0:4], "rpof", "om.0")
+    iota("i.pid", T.pid[:, 0:256], [[1, 256]], 256 * mate1, 0, True)
+    iota("i.idw1", T.idw1[:, 64:128], [[1, 64]], 0, 0, True)
+
+    fresh(0)
+    mm("t.sN", 0, 128, T.qu1c[:], T.qu1s[:], T.hold0c[:, 0:128], T.hold0s[:, 0:128], "q.n0", "sg.A")
+    merge(0, 0, 0, 160, *X)
+    ts("w.N", T.wn[:], T.ps0[:, 0:64], 0.0, 64.0, A.is_lt, A.mult, "t.sN")
+    merge(0, 1, 160, 192, *X)
+    tc("w.1", T.w1[:, 16:352].indirect(T.offm0[:, 0:4]), T.wn[:], "w.N", "w.1x", "om.0")
+    merge(0, 2, 192, 224, *X)
+    scan("f.1", T.f1[:, 0:257], T.w1[:, 16:273], T.w1[:, 15:272], 0.0, A.add, A.add, "w.1", "m.a1", "m.b1")
+
+    send("g.cnt1", mate1, T.cnt1[:, 0:1], T.f1[:, 256:257], "rcnt1", "f.1")
+    merge(0, 3, 224, 256, *X)
+    act("id.p", T.ptmp[:], T.row[:].indirect(T.lin2[:, 0:4]), AF.Copy, "A.lst", "i.row", bias=float(256 * far))
+    act("id.a", T.idw0[:, 0:64], T.row[:].indirect(T.lin[:, 0:4]), AF.Copy, "A.lst", "i.row", "i.idw0", bias=float(256 * mate0))
+    lists(1)
+    M = tuple("mg0%d%s" % (i, k) for i in range(4) for k in "cs")
+    pick("pk1", T.snd1c[:], T.snd1s[:], T.hold1c[:, 128:384], T.hold1s[:, 128:384], T.off1[:, 0:4], ("ov.1", "os.1") + M)
+    send("g.cod1", mate1, u8(T.zc[:, 192:256]), u8(T.snd1c[:, 0:64]), "rcod1", "pk1c")
+    send("g.scl1", mate1, T.zs[:, 192:256], T.snd1s[:, 0:64], "rscl1", "pk1s")
+    send("g.lst1", mate1, T.lin1[:], T.off1[:, 0:4], "rlst1", "ov.1", "os.1")
+    escan(1)
+    quant("q.v", T.qvc[:], T.qvs[:], T.vt[:], "ld.v")
+    mm("t.y", 3, 256, T.qvc[:], T.qvs[:], T.hold1c[:, 128:384], T.hold1s[:, 128:384], "q.v", *M)
+    gap4(1)
+    for i in range(4):
+        expert(1, i)
+    laid(1)
+    settle(1, 0)
+    gap16(1)
+    settle(1, 2)
+    tc("id.q", T.pid[:, 0:336].indirect(T.pof[:, 0:4]), T.ptmp[:], "A.pof", "id.p", "i.pid")
+    for part in range(3, 6):
+        settle(1, part)
+    ts("ks", T.ksb[:], T.th[:], 0.0078125, None, A.mult, None, "th.0", "th.1")
+    act("id.m", T.idw1[:, 128:384], T.idw0[:].indirect(T.offm0[:, 4:20]), AF.Copy, "id.a", "i.idw0", "om.0")
+    act("y.m", T.yrow[:, 0:256], T.ps3[:, 0:256], AF.Copy, "t.y")
+    fresh(1, lambda: act("id.n", T.idw1[:, 0:64], T.pid[:, 0:256].indirect(T.lin1[:, 0:4]), AF.Copy, "id.q", "A.lst1"))
+    act("id.f", T.idf[:], T.idw1[:].indirect(T.offm1[:, 4:20]), AF.Copy, "id.m", "id.n", "i.idw1", "om.1")
+    mm("t.yn", 1, 128, T.qvc[:], T.qvs[:], T.hold1c[:, 0:128], T.hold1s[:, 0:128], "q.n1", "q.v", "w.B")
+    act("y.n", T.yn[:], T.ps1[:, 0:64], AF.Copy, "t.yn")
+    merge(1, 0, 0, 256, *M)
+    tc("y.s", T.yrow[:, 0:336].indirect(T.offm1[:, 0:4]), T.yn[:], "y.n", "y.m", "om.1")
+
+    move("st.k", Y, T.ks[0:1, 0:2], T.ksb[0:1, 0:2], "ks")
+    move("st.i", Y, T.ids[0:1, :], T.idf[0:1, :], "id.f")
+    move("st.c", Y, T.oc[:, :], u8(T.finc[:, 0:256]), "mg10c")
+    move("st.y", Y, T.y[:, :], T.yrow[:, 0:256], "y.s")
+    for k in range(4):
+        move("st.s%d" % k, S if k < 3 else Y, T.osc[4 * k:4 * k + 4, 0:256], T.fins[32 * k:32 * k + 4, 0:256], "mg10s")
+    op("end", Y, None, "st.k", "st.i", "st.c", "st.y", "st.s0", "st.s1", "st.s2", "st.s3")
+
+    qs = (g, V, S, P, Y)
+    known, seen, waits, needed = [set() for _ in qs], {}, [], set()
+
+    def number(q):
+        return [i for i in range(5) if qs[i] is q][0]
+    for name, q, fn, deps, dma in ops:
+        i, w = number(q), []
+        for dep in deps:
+            if dep not in known[i]:
+                w.append(dep)
+                known[i] |= {dep} | seen.get(dep, set())
+                needed.add(dep)
+        seen[name] = set(known[i])
+        waits.append(w)
+    pool, mark = [], {e: arrive[e] for e in arrive}
+    for name, q, fn, deps, dma in ops:
+        if name in needed:
+            i = number(q)
+            old = [s for s in pool if not dma and s[0] == i and s[2] in seen[name]]
+            if old:
+                old[0][2], old[0][3] = name, old[0][3] + 1
+                mark[name] = (old[0][1], old[0][3])
+            else:
+                pool.append([-1 if dma else i, "s%d" % len(pool), name, 16 if dma else 1])
+                mark[name] = (pool[-1][1], pool[-1][3])
+    for (name, q, fn, deps, dma), w in zip(ops, waits):
+        for dep in w:
+            q.wait_ge(T.sem[mark[dep][0]], mark[dep][1])
+        if fn is not None:
+            ins = fn()
+            if name in needed:
+                ins.then_inc(T.sem[mark[name][0]], 16 if dma else 1)
+    g.wait_ge(T.sem["lall"], local["lall"])

@@ -1,4 +1,3 @@
-from concourse.bass import DstId, RemoteDMATransfer
 from concourse.mybir import dt, AluOpType as A, ActivationFunctionType as AF
 
 F8, BF = "float8_e4m3fn_x4", "bfloat16"
@@ -9,32 +8,31 @@ def _sb(n, t="float32"):
 
 
 SCRATCH = {
-    "cna": _sb(1), "cnb": _sb(1, BF), "cnta": _sb(1), "cntb": _sb(1, BF), "cnt1": _sb(1, BF),
-    "lin": _sb(4, "uint16"), "lin2": _sb(4, "uint16"), "pof": _sb(4, "uint16"),
-    "lin1": _sb(4, "uint16"), "offd": _sb(16, "uint16"), "pidx": _sb(2, "int32"), "pand": _sb(2, "int32"), "pand2": _sb(2, "int32"),
+    "cnt0": _sb(1, BF), "cnt1": _sb(1, BF), "pof": _sb(8, "uint16"), "lin1": _sb(4, "uint16"), "offd": _sb(16, "uint16"),
+    "pidx": _sb(2, "int32"), "pand": _sb(2, "int32"), "r32": _sb(16, "int32"),
 }
-for _n, _k in dict(ub=8, xt=1024, wt=4096, vt=512, ut0=512, ut1=512, zt=512, ones=128, h0=512, h1=512, w0=288, w1=352, wn=64,
-                   sig=256, siga=128).items():
+for _n, _k in dict(ub=8, xt=1024, wt=4096, vt=512, ut0=512, ut1=512, hz=768, w0=288, w1=352, wn=64, sig=256, dtr=320).items():
     SCRATCH[_n] = _sb(_k, BF)
-for _n, _k in dict(qu0=128, qu1=128, qw=1024, qv=128, hold0=384, hold1=384, fin=256, snd0=64, snd1=64, z=256).items():
+for _n, _k in dict(qu1=128, qw=1024, qv=128, hold0=384, hold1=384, fin=256, snd0=64, snd1=64, z=256).items():
     SCRATCH[_n + "c"], SCRATCH[_n + "s"] = _sb(_k, F8), _sb(_k, "uint8")
-for _n, _k in dict(pq=2, p31=2, r16=16, r32=16, jw=16, bias=2, lo=2, hi=2, ini=2, alt=20, acnt=1, th=2, ksb=2, row=256, pid=336,
+for _n, _k in dict(pq=2, r16=16, jw=16, bias=2, lo=2, hi=2, ini=2, th=2, ksb=2, pid=336, d0=40, d1=40,
                    ptmp=64, idw0=384, idw1=384, idf=256, yrow=336, yn=64).items():
     SCRATCH[_n] = _sb(_k)
 for _b in "01":
-    for _n, _k in dict(f=272, junk=256, clip=256, sums=256, wb=256, e=256, dup=256, dtr=256).items():
+    for _n, _k in dict(f=272, junk=256, clip=256, sums=256, wb=256, e=256, dup=256).items():
         SCRATCH[_n + _b] = _sb(_k, BF)
-    for _n, _k in dict(acc=2, lf=4, gap=20, sel=20, mov=20, res=20).items():
+    for _n, _k in dict(acc=2, res=40).items():
         SCRATCH[_n + _b] = _sb(_k)
-    SCRATCH["off" + _b], SCRATCH["offm" + _b] = _sb(4, "uint16"), _sb(20, "uint16")
+    SCRATCH["off" + _b], SCRATCH["offm" + _b] = _sb(4, "uint16"), _sb(28, "uint16")
 for _b in range(8):
     SCRATCH["ps%d" % _b] = ("psum", [128, 512], "float32")
 
-REMOTE = ["rcnta", "rcntb", "rcod0", "rscl0", "rlst", "rpof", "rcnt1", "rlst1", "rcod1", "rscl1", "lall", "lcnt", "go"]
+REMOTE = ["rcnt0", "rcod0", "rscl0", "rlst", "rpof", "rcnt1", "rlst1", "rcod1", "rscl1", "lall", "lcnt", "go"]
 POOL = 80
 SEMAPHORES = REMOTE + ["s%d" % _i for _i in range(POOL)]
 Z = (0, 128)
 NEW = (0, 64)
+UNIT = 1024.0
 
 
 def rank_program(g, core, T, topo):
@@ -51,12 +49,10 @@ def rank_program(g, core, T, topo):
 
     def eng(a, b):
         return len(topo.engines(cores[a], cores[b]))
-    arrive = {"A.lst": ("rlst", eng(mate0, rank) + eng(far, rank)), "A.pof": ("rpof", eng(mate1, rank)),
-              "A.lst1": ("rlst1", eng(mate1, rank)), "A.cnt1": ("rcnt1", eng(mate1, rank)),
-              "A.cnta": ("rcnta", eng(mate0, rank)), "A.cntb": ("rcntb", eng(mate0, rank)),
+    arrive = {"A.lst": ("rlst", eng(mate0, rank)), "A.pof": ("rpof", eng(mate1, rank)), "A.lst1": ("rlst1", eng(mate1, rank)),
               "E.go": ("go", 1), "L.cnt": ("lcnt", eng(rank, mate0))}
     for b, m in ((0, mate0), (1, mate1)):
-        for kind in ("cod", "scl"):
+        for kind in ("cnt", "cod", "scl"):
             arrive["A.%s%d" % (kind, b)] = ("r%s%d" % (kind, b), eng(m, rank))
 
     def send(name, to, dst, src, sem, *deps, lsem="lall"):
@@ -80,9 +76,6 @@ def rank_program(g, core, T, topo):
         else:
             op(name, V, lambda: V.tensor_scalar(out, in0, s1, s2, o0, o1), *deps)
 
-    def tt(name, out, a, b, o, *deps):
-        op(name, V, lambda: V.tensor_tensor(out, a, b, o), *deps)
-
     def tc(name, out, in_, *deps):
         op(name, V, lambda: V.tensor_copy(out, in_), *deps)
 
@@ -98,11 +91,13 @@ def rank_program(g, core, T, topo):
     def move(name, q, out, in_, *deps):
         op(name, q, lambda: q.dma_start(out, in_), *deps, dma=True)
 
-    def iota(name, out, pattern, base, cm, flag):
+    def iota(name, out, pattern, base, cm, flag, *deps):
         if flag:
-            op(name, g, lambda: g.iota(out, pattern, base, cm, allow_small_or_imprecise_dtypes=True))
+            op(name, g, lambda: g.iota(out, pattern, base, cm, allow_small_or_imprecise_dtypes=True), *deps)
         else:
-            op(name, g, lambda: g.iota(out, pattern, base, cm))
+            op(name, g, lambda: g.iota(out, pattern, base, cm), *deps)
+
+    zero = T.hz[:, 256:384]
 
     move("ld.u", S, T.ub[:, 0:8], T.u[:, 0:8])
     move("ld.xA", Y, T.xt[:, 0:512], T.x[:, 0:512])
@@ -111,44 +106,38 @@ def rank_program(g, core, T, topo):
 
     iota("i.p", T.pidx[:], [[0, 2]], 0, 1, False)
     iota("i.r16", T.r16[:], [[16, 16]], 0, 0, True)
-    iota("i.r32", T.r32[:], [[32, 8], [0, 2]], 0, 0, True)
-    op("m.ones", V, lambda: V.memset(T.ones[:], 1.0))
-    op("m.zt", V, lambda: V.memset(T.zt[:], 0.0))
+    iota("m.a0", T.w0[:, 15:273:257], [[0, 2]], 0, 0, True)
+    iota("m.a1", T.w1[:, 15:273:257], [[0, 2]], 0, 0, True)
+    iota("c.d0", T.d0[:, 0:40:2], [[0, 20]], 4, 0, True)
+    for a in range(4):
+        iota("i.r32%d" % a, T.r32[32 * a:32 * a + 32, :], [[32, 8], [0, 2]], 0, 1, False, "i.p", "i.r16", "m.a0", "m.a1", "c.d0")
+    R32 = tuple("i.r32%d" % a for a in range(4))
+    op("m.zt", V, lambda: V.memset(T.hz[:, 256:512], 0.0))
     ts("c.and", T.pand[:], T.pidx[:], 15, None, A.bitwise_and, None, "i.p")
-    ts("c.and2", T.pand2[:], T.pidx[:], 31, None, A.bitwise_and, None, "i.p")
     tc("c.pq", T.pq[:], T.pand[:], "c.and")
-    tc("c.p31", T.p31[:], T.pand2[:], "c.and2")
     ts("c.jw", T.jw[:], T.r16[:], T.pq[:, 0:1], None, A.add, None, "c.pq", "i.r16")
-    ts("c.offd", T.offd[:], T.r32[:], T.p31[:, 0:1], None, A.add, None, "c.p31", "i.r32")
-    quant("q.z", T.zc[:, 64:192], T.zs[:, 64:192], T.zt[:], "m.zt")
-    for b in range(2):
-        act("m.h%d" % b, T["h%d" % b][:, 256:512], T.zt[:, 0:256], AF.Copy, "m.zt")
-    for b, w, k in ((0, T.w0, 288), (1, T.w1, 280)):
-        act("m.a%d" % b, w[:, 0:16], T.zt[:, 0:16], AF.Copy, "m.zt")
-        act("m.b%d" % b, w[:, 272:k], T.zt[:, 0:k - 272], AF.Copy, "m.zt")
 
     for t in range(3):
-        ts("u0.%d" % t, T.ut0[:, t:512:4], T.ones[:, 0:128], T.ub[:, t:t + 1], None, A.mult, None, "ld.u", "m.ones")
-    act("u0.3", T.ut0[:, 3:512:4], T.zt[:, 0:128], AF.Identity, "ld.u", "m.zt", bias=T.ub[:, 3:4])
+        ts("u0.%d" % t, T.ut0[:, t:512:4], zero, T.ub[:, t:t + 1], None, A.add, None, "ld.u", "m.zt")
+    act("u0.3", T.ut0[:, 3:512:4], zero, AF.Identity, "ld.u", "m.zt", bias=T.ub[:, 3:4])
     act("c.bias", T.bias[:], T.jw[:, 2:4], AF.Copy, "c.jw", scale=128.0, bias=64.0)
     act("c.lo", T.lo[:], T.jw[:, 0:2], AF.Copy, "c.jw", scale=128.0)
     act("c.hi", T.hi[:], T.jw[:, 0:2], AF.Copy, "c.jw", scale=128.0, bias=128.0)
     act("c.ini", T.ini[:], T.jw[:, 0:2], AF.Copy, "c.jw", scale=16384.0, bias=16384.0)
     for t in range(4):
-        act("u1.%d" % t, T.ut1[:, t:512:4], T.zt[:, 0:128], AF.Identity, "ld.u", "m.zt", bias=T.ub[:, 4 + t:5 + t])
-    quant("q.u0", T.qu0c[:], T.qu0s[:], T.ut0[:], "u0.0", "u0.1", "u0.2", "u0.3")
+        act("u1.%d" % t, T.ut1[:, t:512:4], zero, AF.Identity, "ld.u", "m.zt", bias=T.ub[:, 4 + t:5 + t])
+    quant("q.u0", T.zc[:, 64:192], T.zs[:, 64:192], T.ut0[:], "u0.0", "u0.1", "u0.2", "u0.3")
 
     X = ("q.xA", "q.xB")
     quant("q.xA", T.hold0c[:, 128:256], T.hold0s[:, 128:256], T.xt[:, 0:512], "ld.xA")
-    mm("t.sA", 0, 128, T.qu0c[:], T.qu0s[:], T.hold0c[:, 128:256], T.hold0s[:, 128:256], "q.u0", "q.xA")
-    act("sg.A", T.siga[:], T.ps0[:, 0:128], AF.Sign, "t.sA", scale=-1.0)
-    act("w.A", T.w0[:, 16:144], T.siga[:], AF.Relu, "sg.A", scale=64.0, accum_out=T.cna[:, 0:1])
+    mm("t.sA", 0, 128, T.zc[:, 64:192], T.zs[:, 64:192], T.hold0c[:, 128:256], T.hold0s[:, 128:256], "q.u0", "q.xA")
     quant("q.xB", T.hold0c[:, 256:384], T.hold0s[:, 256:384], T.xt[:, 512:1024], "ld.xB")
-    mm("t.sB", 1, 128, T.qu0c[:], T.qu0s[:], T.hold0c[:, 256:384], T.hold0s[:, 256:384], "q.u0", "q.xB")
+    mm("t.sB", 1, 128, T.zc[:, 64:192], T.zs[:, 64:192], T.hold0c[:, 256:384], T.hold0s[:, 256:384], "q.u0", "q.xB")
+    ts("w.A", T.w0[:, 16:144], T.ps0[:, 0:128], 0.0, 64.0, A.is_lt, A.mult, "t.sA")
     scan("f.A", T.f0[:, 0:128], T.w0[:, 16:144], T.w0[:, 15:143], 0.0, A.add, A.add, "w.A", "m.a0")
     act("wb.A", T.wb0[:, 0:128], T.w0[:, 15:143], AF.Copy, "w.A", "m.a0", scale=1.015625)
     ts("w.B", T.w0[:, 144:272], T.ps1[:, 0:128], 0.0, 64.0, A.is_lt, A.mult, "t.sB")
-    scan("f.0", T.f0[:, 128:257], T.w0[:, 144:273], T.w0[:, 143:272], T.f0[:, 127:128], A.add, A.add, "w.B", "f.A", "m.b0")
+    scan("f.0", T.f0[:, 128:257], T.w0[:, 144:273], T.w0[:, 143:272], T.f0[:, 127:128], A.add, A.add, "w.B", "f.A")
 
     def lists(b):
         f, acc, cl, su, off, junk = (T[k % b] for k in ("f%d", "acc%d", "clip%d", "sums%d", "off%d", "junk%d"))
@@ -159,11 +148,9 @@ def rank_program(g, core, T, topo):
         for m in range(2):
             ts("pm%d.%d" % (m, b), cl[:, 128 * m:128 * m + 128], f[:, 1:256:2], T.lo[:, m:m + 1], T.hi[:, m:m + 1], A.max, A.min,
                n, "c.lo", "c.hi")
-        if not b:
-            ts("n.B", T.cnb[:], f[:, 256:257], T.cna[:, 0:1], T.cna[:, 0:1], A.subtract, A.subtract, n, "w.A")
         for m in range(2):
-            scan("pc%d.%d" % (m, b), su[:, 128 * m:128 * m + 128], T.ones[:, 0:128], cl[:, 128 * m:128 * m + 128],
-                 T.ini[:, m:m + 1], A.mult, A.subtract, "pm%d.%d" % (m, b), "c.ini")
+            scan("pc%d.%d" % (m, b), su[:, 128 * m:128 * m + 128], zero, cl[:, 128 * m:128 * m + 128],
+                 T.ini[:, m:m + 1], A.add, A.subtract, "pm%d.%d" % (m, b), "c.ini")
         p = 0 if b else 128
         act("wb.B%d" % b, T["wb%d" % b][:, p:256], T["w%d" % b][:, 15 + p:271], AF.Copy, n, scale=1.015625)
         ts("os.%d" % b, off[:, 2:4], acc[:, 0:2], 111.0, 144.0, A.min, A.add, "ps0.%d" % b, "ps1.%d" % b)
@@ -179,114 +166,97 @@ def rank_program(g, core, T, topo):
              T["offm%d" % b][:, 4 + p // 16:4 + q // 16], ("om.%d" % b, "q.n%d" % b) + deps)
 
     def escan(b):
+        old = ("sc.0",) if b else ()
         scan("e.%d" % b, T["e%d" % b][:], T["wb%d" % b][:], T["w%d" % b][:, 16:272], 64.0, A.add, A.subtract, "wb.B%d" % b,
              "f.%d" % b, *(() if b else ("wb.A",)))
-        tc("lf.%d" % b, T["lf%d" % b][:], T["off%d" % b][:, 0:4], "ov.%d" % b, "os.%d" % b)
+        if not b:
+            tc("c.offd", T.offd[:], T.r32[:], *R32)
+        act("a2.%d" % b, T.d0[:, 33:36:2], T["sums%d" % b][:, 127:256:128], AF.Copy, "pc0.%d" % b, "pc1.%d" % b, *old,
+            scale=1 / (64 * UNIT))
+        act("a4.%d" % b, T.d0[:, 37:40:2], T["acc%d" % b][:, 0:2], AF.Copy, "ps0.%d" % b, "ps1.%d" % b, *old,
+            scale=1 / UNIT, bias=144 / UNIT)
         act("dup.%d" % b, T["dup%d" % b][:], T["e%d" % b][:, 0:256].indirect(T.offd[:, 0:16]), AF.Copy, "e.%d" % b, "c.offd")
 
-    def gap4(b):
-        tt("g4.%d" % b, T["gap%d" % b][:, 0:4], T["lf%d" % b][:], T.alt[:, 0:4], A.subtract, "lf.%d" % b, "c.alt0")
-
     def laid(b):
-        op("tr.%d" % b, V, lambda: V.transpose(T["dtr%d" % b][:], T["dup%d" % b][:]), "dup.%d" % b)
+        op("tr.%d" % b, V, lambda: V.transpose(T.dtr[:, 0:256], T["dup%d" % b][:]), "dup.%d" % b, *(("sc.0",) if b else ()))
 
-    def gap16(b):
-        tt("g16.%d" % b, T["gap%d" % b][:, 4:20], T["dtr%d" % b][:, 0:256:16], T.alt[:, 4:20], A.subtract, "tr.%d" % b, "c.alt1")
+    def a16(b):
+        act("a16.%d" % b, T.d0[:, 1:32:2], T.dtr[:, 0:256:16], AF.Copy, "tr.%d" % b, scale=1 / UNIT, bias=NEW[b] / UNIT)
 
     def settle(b, part):
-        own = T["f%d" % b][:, 256:257]
         if part == 0:
-            if b:
-                ts("th.1", T.th[:, 1:2], T.cnt1[:, 0:1], own, 8192.0, A.min, A.min, "A.cnt1", "f.1")
-            else:
-                ts("nn.0", T.acnt[:], T.cntb[:, 0:1], T.cnta[:, 0:1], T.cnta[:, 0:1], A.add, A.add, "A.cnta", "A.cntb")
-        if part == 1 and not b:
-            ts("th.0", T.th[:, 0:1], T.acnt[:], own, 8192.0, A.min, A.min, "nn.0", "f.0")
+            ts("th.%d" % b, T.th[:, b:b + 1], T["cnt%d" % b][:, 0:1], T["f%d" % b][:, 256:257], 8192.0, A.min, A.min,
+               "A.cnt%d" % b, "f.%d" % b)
+        if part == 1:
+            ts("sel.%d" % b, T.d1[:, 0:40:2], T.dtr[:, 0:320:16], 128.0, T.th[:, b:b + 1], A.mult, A.is_ge, "th.%d" % b,
+               "tr.%d" % b, "c.idx")
         if part == 2:
-            ts("s4.%d" % b, T["sel%d" % b][:, 0:4], T.jw[:, 0:4], 128.0, T.th[:, b:b + 1], A.mult, A.is_lt, "th.%d" % b, "c.jw")
-            ts("s16.%d" % b, T["sel%d" % b][:, 4:20], T["dtr%d" % b][:, 0:256:16], 128.0, T.th[:, b:b + 1], A.mult, A.is_lt,
-               "th.%d" % b, "tr.%d" % b)
+            scan("sc.%d" % b, T["res%d" % b][:], T.d0[:], T.d1[:], 0.0, A.add, A.min, "sel.%d" % b, "a16.%d" % b, "a2.%d" % b,
+                 "a4.%d" % b, "c.d0", "c.alt0", "c.alt1")
         if part == 3:
-            tt("mv.%d" % b, T["mov%d" % b][:], T["sel%d" % b][:], T["gap%d" % b][:], A.mult, "s4.%d" % b, "s16.%d" % b,
-               "g4.%d" % b, "g16.%d" % b)
-        if part == 4:
-            tt("rs.%d" % b, T["res%d" % b][:], T["mov%d" % b][:], T.alt[:], A.add, "mv.%d" % b, "c.alt0", "c.alt1")
-        if part == 5:
-            tc("om.%d" % b, T["offm%d" % b][:], T["res%d" % b][:], "rs.%d" % b)
+            ts("om.%d" % b, T["offm%d" % b][:, 4:24], T["res%d" % b][:, 1:40:2], UNIT, None, A.mult, None, "sc.%d" % b)
 
     def expert(b, i):
         a, c = 512 * b + 128 * i, 2048 * b + 512 * i
         quant("q.w%d%d" % (i, b), T.qwc[:, a:a + 128], T.qws[:, a:a + 128], T.wt[:, c:c + 512], "ld.w%d" % b)
 
-    def fresh(b, between=None):
-        h, hold, z = T["h%d" % b], "hold%d" % b, Z[b]
+    def fresh(b):
+        h, hold, z, o = T.hz, "hold%d" % b, Z[b], 512 * b
         for i in range(4):
             a = 512 * b + 128 * i
             mm("R%d.%d" % (i, b), 4 + i, 128, T.qwc[:, a:a + 128], T.qws[:, a:a + 128], T.zc[:, z:z + 128], T.zs[:, z:z + 128],
-               "q.w%d%d" % (i, b), "q.z", "A.cod%d" % b, "A.scl%d" % b, *(("K%d.0" % i,) if b else ()))
+               "q.w%d%d" % (i, b), "q.u0", "A.cod%d" % b, "A.scl%d" % b, *(("K%d.0" % i,) if b else ()))
         for i in range(4):
             r = T["ps%d" % (4 + i)][:, NEW[b]:NEW[b] + 64]
             if i == 3:
-                ts("K%d.%d" % (i, b), h[:, i:256:4], r, 0.0625, None, A.mult, None, "R%d.%d" % (i, b))
+                ts("K%d.%d" % (i, b), h[:, o + i:o + 256:4], r, 0.0625, None, A.mult, None, "R%d.%d" % (i, b))
             else:
-                act("K%d.%d" % (i, b), h[:, i:256:4], r, AF.Copy, "R%d.%d" % (i, b), scale=0.0625)
-                if i == 0 and between is not None:
-                    between()
-        quant("q.n%d" % b, T[hold + "c"][:, 0:128], T[hold + "s"][:, 0:128], h[:],
-              *["K%d.%d" % (i, b) for i in range(4)], "m.h%d" % b)
+                act("K%d.%d" % (i, b), h[:, o + i:o + 256:4], r, AF.Copy, "R%d.%d" % (i, b), scale=0.0625)
+        quant("q.n%d" % b, T[hold + "c"][:, 0:128], T[hold + "s"][:, 0:128], h[:, 256 * b:256 * b + 512],
+              *["K%d.%d" % (i, b) for i in range(4)], "m.zt")
 
-    send("g.cnta", mate0, T.cnta[:, 0:1], T.cna[:, 0:1], "rcnta", "w.A", lsem="lcnt")
+    send("g.cnt0", mate0, T.cnt0[:, 0:1], T.f0[:, 256:257], "rcnt0", "f.0", lsem="lcnt")
     lists(0)
-    send("g.cntb", mate0, T.cntb[:, 0:1], T.cnb[:, 0:1], "rcntb", "n.B")
     pick("pk0", T.snd0c[:], T.snd0s[:], T.hold0c[:, 128:384], T.hold0s[:, 128:384], T.off0[:, 0:4], ("ov.0", "os.0") + X)
     send("g.cod0", mate0, u8(T.zc[:, 0:64]), u8(T.snd0c[:, 0:64]), "rcod0", "pk0c")
     send("g.scl0", mate0, T.zs[:, 0:64], T.snd0s[:, 0:64], "rscl0", "pk0s")
-    to = [topo.addr(cores[r]) for r in (mate0, far)]
-    local["lall"] += eng(rank, mate0)
-    op("g.lst", g, lambda: g.remote_dma_fused([RemoteDMATransfer(
-        dst_ids=[DstId(rid=a[0], pnc=a[1]) for a in to],
-        dma_engine_mask=topo.mask(core, cores[mate0]) & topo.mask(core, cores[far]),
-        remote_sem=T.sem["rlst"], srcs=[T.off0[:, 0:4]], dsts=[T.lin[:], T.lin2[:]])], local_sem=T.sem["lall"]), "ov.0", "os.0")
+    send("g.lst", mate0, T.offm0[:, 24:28], T.off0[:, 0:4], "rlst", "ov.0", "os.0")
     op("g.go", g, lambda: g.sem_inc(T.sem["go"], 1))
-    move("ld.v", Y, T.vt[:], T.v[:], "E.go", "L.cnt")
-    move("ld.w1", Y, T.wt[:, 2048:4096], T.w[:, 2048:4096])
-    iota("i.row", T.row[:], [[1, 256]], 0, 0, True)
-    iota("i.idw0", T.idw0[:], [[1, 384]], 256 * rank - 128, 0, True)
+    move("ld.w1", Y, T.wt[:, 2048:4096], T.w[:, 2048:4096], "E.go", "L.cnt")
+    move("ld.v", Y, T.vt[:], T.v[:])
+    iota("i.idw0", T.idw0[:], [[1, 384]], 256 * rank - 128, 0, True, *R32)
+    iota("i.pid", T.pid[:, 0:256], [[1, 256]], 256 * mate1, 0, True)
+    iota("i.idw1", T.idw1[:, 0:64], [[1, 64]], 0, 0, True)
 
-    act("c.alt0", T.alt[:, 0:4], T.jw[:, 0:4], AF.Copy, "c.jw", bias=264.0)
-    act("c.alt1", T.alt[:, 4:20], T.jw[:], AF.Copy, "c.jw", bias=128.0)
+    act("c.alt1", T.d1[:, 1:32:2], T.jw[:], AF.Copy, "c.jw", scale=1 / UNIT, bias=128 / UNIT)
     escan(0)
+    act("c.alt0", T.d1[:, 33:40:2], T.jw[:, 0:4], AF.Copy, "c.jw", scale=1 / UNIT, bias=264 / UNIT)
+    act("c.idx", T.dtr[:, 256:320:16], T.jw[:, 0:4], AF.Copy, "c.jw")
     quant("q.u1", T.qu1c[:], T.qu1s[:], T.ut1[:], "u1.0", "u1.1", "u1.2", "u1.3")
     mm("t.s1", 2, 256, T.qu1c[:], T.qu1s[:], T.hold0c[:, 128:384], T.hold0s[:, 128:384], "q.u1", *X)
     act("sg.1", T.sig[:], T.ps2[:, 0:256], AF.Sign, "t.s1", scale=-1.0)
-    act("w.1x", T.w1[:, 16:272], T.sig[:], AF.Relu, "sg.1", scale=64.0)
-    expert(0, 0)
-    gap4(0)
-    expert(0, 1)
-    expert(0, 2)
-    expert(0, 3)
+    for i in range(4):
+        expert(0, i)
     laid(0)
-    settle(0, 0)
-    gap16(0)
-    for part in range(1, 6):
+    a16(0)
+    act("w.1x", T.w1[:, 16:272], T.sig[:], AF.Relu, "sg.1", scale=64.0)
+    for part in range(4):
         settle(0, part)
-    send("g.pof", mate1, T.pof[:], T.offm0[:, 0:4], "rpof", "om.0")
-    iota("i.pid", T.pid[:, 0:256], [[1, 256]], 256 * mate1, 0, True)
-    iota("i.idw1", T.idw1[:, 64:128], [[1, 64]], 0, 0, True)
+    send("g.pof", mate1, T.pof[:], T.offm0[:, 20:28], "rpof", "om.0", "A.lst")
 
     fresh(0)
-    mm("t.sN", 0, 128, T.qu1c[:], T.qu1s[:], T.hold0c[:, 0:128], T.hold0s[:, 0:128], "q.n0", "sg.A")
+    mm("t.sN", 0, 128, T.qu1c[:], T.qu1s[:], T.hold0c[:, 0:128], T.hold0s[:, 0:128], "q.n0", "w.A")
     merge(0, 0, 0, 160, *X)
     ts("w.N", T.wn[:], T.ps0[:, 0:64], 0.0, 64.0, A.is_lt, A.mult, "t.sN")
     merge(0, 1, 160, 192, *X)
-    tc("w.1", T.w1[:, 16:352].indirect(T.offm0[:, 0:4]), T.wn[:], "w.N", "w.1x", "om.0")
+    tc("w.1", T.w1[:, 16:352].indirect(T.offm0[:, 20:24]), T.wn[:], "w.N", "w.1x", "om.0")
     merge(0, 2, 192, 224, *X)
-    scan("f.1", T.f1[:, 0:257], T.w1[:, 16:273], T.w1[:, 15:272], 0.0, A.add, A.add, "w.1", "m.a1", "m.b1")
+    scan("f.1", T.f1[:, 0:257], T.w1[:, 16:273], T.w1[:, 15:272], 0.0, A.add, A.add, "w.1", "m.a1")
 
     send("g.cnt1", mate1, T.cnt1[:, 0:1], T.f1[:, 256:257], "rcnt1", "f.1")
     merge(0, 3, 224, 256, *X)
-    act("id.p", T.ptmp[:], T.row[:].indirect(T.lin2[:, 0:4]), AF.Copy, "A.lst", "i.row", bias=float(256 * far))
-    act("id.a", T.idw0[:, 0:64], T.row[:].indirect(T.lin[:, 0:4]), AF.Copy, "A.lst", "i.row", "i.idw0", bias=float(256 * mate0))
+    act("id.a", T.idw0[:, 0:64], T.idw0[:, 128:384].indirect(T.offm0[:, 24:28]), AF.Copy, "A.lst", "i.idw0",
+        bias=float(256 * (mate0 - rank)))
     lists(1)
     M = tuple("mg0%d%s" % (i, k) for i in range(4) for k in "cs")
     pick("pk1", T.snd1c[:], T.snd1s[:], T.hold1c[:, 128:384], T.hold1s[:, 128:384], T.off1[:, 0:4], ("ov.1", "os.1") + M)
@@ -296,25 +266,26 @@ def rank_program(g, core, T, topo):
     escan(1)
     quant("q.v", T.qvc[:], T.qvs[:], T.vt[:], "ld.v")
     mm("t.y", 3, 256, T.qvc[:], T.qvs[:], T.hold1c[:, 128:384], T.hold1s[:, 128:384], "q.v", *M)
-    gap4(1)
     for i in range(4):
         expert(1, i)
-    laid(1)
     settle(1, 0)
-    gap16(1)
-    settle(1, 2)
-    tc("id.q", T.pid[:, 0:336].indirect(T.pof[:, 0:4]), T.ptmp[:], "A.pof", "id.p", "i.pid")
-    for part in range(3, 6):
-        settle(1, part)
-    ts("ks", T.ksb[:], T.th[:], 0.0078125, None, A.mult, None, "th.0", "th.1")
-    act("id.m", T.idw1[:, 128:384], T.idw0[:].indirect(T.offm0[:, 4:20]), AF.Copy, "id.a", "i.idw0", "om.0")
+    laid(1)
+    act("id.p", T.ptmp[:], T.idw0[:, 128:384].indirect(T.pof[:, 4:8]), AF.Copy, "A.pof", "i.idw0", bias=float(256 * (far - rank)))
     act("y.m", T.yrow[:, 0:256], T.ps3[:, 0:256], AF.Copy, "t.y")
-    fresh(1, lambda: act("id.n", T.idw1[:, 0:64], T.pid[:, 0:256].indirect(T.lin1[:, 0:4]), AF.Copy, "id.q", "A.lst1"))
+    a16(1)
+    settle(1, 1)
+    tc("id.q", T.pid[:, 0:336].indirect(T.pof[:, 0:4]), T.ptmp[:], "A.pof", "id.p", "i.pid")
+    settle(1, 2)
+    settle(1, 3)
+    act("id.m", T.idw1[:, 128:384], T.idw0[:].indirect(T.offm0[:, 4:20]), AF.Copy, "id.a", "i.idw0", "om.0")
+    fresh(1)
+    act("id.n", T.idw1[:, 64:128], T.pid[:, 0:256].indirect(T.lin1[:, 0:4]), AF.Copy, "id.q", "A.lst1")
+    act("ks", T.ksb[:], T.th[:], AF.Copy, "th.0", "th.1", scale=0.0078125)
     act("id.f", T.idf[:], T.idw1[:].indirect(T.offm1[:, 4:20]), AF.Copy, "id.m", "id.n", "i.idw1", "om.1")
     mm("t.yn", 1, 128, T.qvc[:], T.qvs[:], T.hold1c[:, 0:128], T.hold1s[:, 0:128], "q.n1", "q.v", "w.B")
-    act("y.n", T.yn[:], T.ps1[:, 0:64], AF.Copy, "t.yn")
+    act("y.n", T.yn[:], T.ps1[:, 64:128], AF.Copy, "t.yn")
     merge(1, 0, 0, 256, *M)
-    tc("y.s", T.yrow[:, 0:336].indirect(T.offm1[:, 0:4]), T.yn[:], "y.n", "y.m", "om.1")
+    tc("y.s", T.yrow[:, 0:336].indirect(T.offm1[:, 20:24]), T.yn[:], "y.n", "y.m", "om.1")
 
     move("st.k", Y, T.ks[0:1, 0:2], T.ksb[0:1, 0:2], "ks")
     move("st.i", Y, T.ids[0:1, :], T.idf[0:1, :], "id.f")

@@ -1,37 +1,34 @@
 from concourse.mybir import dt, AluOpType as A, ActivationFunctionType as AF
 
-F8, BF = "float8_e4m3fn_x4", "bfloat16"
+F8, BF, U16 = "float8_e4m3fn_x4", "bfloat16", "uint16"
 
 
 def _sb(n, t="float32"):
     return ("sbuf", [128, n], t)
 
 
-SCRATCH = {
-    "cnt0": _sb(1, BF), "cnt1": _sb(1, BF), "pof": _sb(8, "uint16"), "lin1": _sb(4, "uint16"), "offd": _sb(16, "uint16"),
-    "pidx": _sb(2, "int32"), "pand": _sb(2, "int32"), "r32": _sb(16, "int32"),
-}
-for _n, _k in dict(ub=8, xt=1024, wt=4096, vt=512, ut0=512, ut1=512, hz=768, w0=288, w1=352, wn=64, sig=256, dtr=320).items():
+SCRATCH = {"pidx": _sb(16, "int32"), "pand": _sb(16, "int32"), "r32": _sb(16, "int32")}
+for _n, _k in dict(pof=8, lin1=4, offd=16, offi=16, off0=4, off1=4, offm0=28, offm1=28).items():
+    SCRATCH[_n] = _sb(_k, U16)
+for _n, _k in dict(cnt0=1, cnt1=1, ub=8, xt=1024, wt=4096, vt=512, ut0=512, ut1=512, hz=768, w0=288, w1=352, wn=64, sig=256,
+                   dtr=320, cap=256).items():
     SCRATCH[_n] = _sb(_k, BF)
 for _n, _k in dict(qu1=128, qw=1024, qv=128, hold0=384, hold1=384, fin=256, snd0=64, snd1=64, z=256).items():
     SCRATCH[_n + "c"], SCRATCH[_n + "s"] = _sb(_k, F8), _sb(_k, "uint8")
-for _n, _k in dict(pq=2, r16=16, jw=16, bias=2, lo=2, hi=2, ini=2, th=2, ksb=2, pid=336, d0=40, d1=40,
-                   ptmp=64, idw0=384, idw1=384, idf=256, yrow=336, yn=64).items():
+for _n, _k in dict(r16=16, jw=16, top=2, ini=2, th=2, tm=2, ksb=2, pid=336, d0=60, d1=60, ptmp=64, idw=384, idf=256,
+                   yrow=336, yn=64, acc0=2, acc1=2, res0=60, res1=60).items():
     SCRATCH[_n] = _sb(_k)
 for _b in "01":
-    for _n, _k in dict(f=272, junk=256, clip=256, sums=256, wb=256, e=256, dup=256).items():
+    for _n, _k in dict(f=272, g=256, junk=256, sums=512, wb=256, e=256, dup=256).items():
         SCRATCH[_n + _b] = _sb(_k, BF)
-    for _n, _k in dict(acc=2, res=40).items():
-        SCRATCH[_n + _b] = _sb(_k)
-    SCRATCH["off" + _b], SCRATCH["offm" + _b] = _sb(4, "uint16"), _sb(28, "uint16")
 for _b in range(8):
     SCRATCH["ps%d" % _b] = ("psum", [128, 512], "float32")
 
 REMOTE = ["rcnt0", "rcod0", "rscl0", "rlst", "rpof", "rcnt1", "rlst1", "rcod1", "rscl1", "lall", "lcnt", "go"]
 POOL = 80
 SEMAPHORES = REMOTE + ["s%d" % _i for _i in range(POOL)]
-Z = (0, 128)
-NEW = (0, 64)
+Z = (128, 0)
+NEW = (64, 0)
 UNIT = 1024.0
 
 
@@ -67,8 +64,9 @@ def rank_program(g, core, T, topo):
     def u32(v):
         return v.bitcast(dt.uint32)
 
-    def mm(name, bank, n, wc, ws, xc, xs, *deps):
-        op(name, P, lambda: P.matmul_mx(T["ps%d" % bank][:, 0:n], wc, ws, xc, xs, True, True), *deps)
+    def mm(name, bank, q, a, x, p, n, *deps):
+        op(name, P, lambda: P.matmul_mx(T["ps%d" % bank][:, 0:n], T[q + "c"][:, a:a + 128], T[q + "s"][:, a:a + 128],
+                                        T[x + "c"][:, p:p + n], T[x + "s"][:, p:p + n], True, True), *deps)
 
     def ts(name, out, in0, s1, s2, o0, o1, *deps):
         if o1 is None:
@@ -85,17 +83,17 @@ def rank_program(g, core, T, topo):
     def act(name, out, in_, fn, *deps, **kw):
         op(name, S, lambda: S.activation(out, in_, fn, **kw), *deps)
 
-    def quant(name, qc, qs, t, *deps):
-        op(name, V, lambda: V.quantize_mx(qc, qs, t), *deps)
+    def quant(name, q, a, t, *deps):
+        op(name, V, lambda: V.quantize_mx(T[q + "c"][:, a:a + 128], T[q + "s"][:, a:a + 128], t), *deps)
 
     def move(name, q, out, in_, *deps):
         op(name, q, lambda: q.dma_start(out, in_), *deps, dma=True)
 
-    def iota(name, out, pattern, base, cm, flag, *deps):
-        if flag:
-            op(name, g, lambda: g.iota(out, pattern, base, cm, allow_small_or_imprecise_dtypes=True), *deps)
-        else:
-            op(name, g, lambda: g.iota(out, pattern, base, cm), *deps)
+    def iota(name, out, pattern, base, *deps):
+        op(name, g, lambda: g.iota(out, pattern, base, 0, allow_small_or_imprecise_dtypes=True), *deps)
+
+    def iotp(name, out, pattern, *deps):
+        op(name, g, lambda: g.iota(out, pattern, 0, 1), *deps)
 
     zero = T.hz[:, 256:384]
 
@@ -103,188 +101,193 @@ def rank_program(g, core, T, topo):
     move("ld.xA", Y, T.xt[:, 0:512], T.x[:, 0:512])
     move("ld.xB", Y, T.xt[:, 512:1024], T.x[:, 512:1024])
     move("ld.w0", Y, T.wt[:, 0:2048], T.w[:, 0:2048])
+    move("ld.v", Y, T.vt[:], T.v[:])
 
-    iota("i.p", T.pidx[:], [[0, 2]], 0, 1, False)
-    iota("i.r16", T.r16[:], [[16, 16]], 0, 0, True)
-    iota("m.a0", T.w0[:, 15:273:257], [[0, 2]], 0, 0, True)
-    iota("m.a1", T.w1[:, 15:273:257], [[0, 2]], 0, 0, True)
-    iota("c.d0", T.d0[:, 0:40:2], [[0, 20]], 4, 0, True)
+    iotp("i.p", T.pidx[:], [[0, 16]])
+    iota("i.r16", T.r16[:], [[16, 16]], 0)
+    iota("m.a0", T.w0[:, 15:273:257], [[0, 2]], 0)
+    iota("m.a1", T.w1[:, 15:273:257], [[0, 2]], 0)
+    iota("c.d0", T.d0[:], [[0, 20], [-2, 3]], 4)
+    iota("c.d1", T.d1[:, 2:60:3], [[0, 20]], 1)
     for a in range(4):
-        iota("i.r32%d" % a, T.r32[32 * a:32 * a + 32, :], [[32, 8], [0, 2]], 0, 1, False, "i.p", "i.r16", "m.a0", "m.a1", "c.d0")
+        iotp("i.r32%d" % a, T.r32[32 * a:32 * a + 32, :], [[32, 8], [0, 2]], "i.p", "i.r16", "m.a0", "m.a1", "c.d0", "c.d1")
     R32 = tuple("i.r32%d" % a for a in range(4))
     op("m.zt", V, lambda: V.memset(T.hz[:, 256:512], 0.0))
+    op("m.one", V, lambda: V.memset(T.junk1[:], 1.0))
     ts("c.and", T.pand[:], T.pidx[:], 15, None, A.bitwise_and, None, "i.p")
-    tc("c.pq", T.pq[:], T.pand[:], "c.and")
-    ts("c.jw", T.jw[:], T.r16[:], T.pq[:, 0:1], None, A.add, None, "c.pq", "i.r16")
+    scan("c.cap", T.cap[:], T.hz[:, 256:512], T.junk1[:], 0.0, A.add, A.subtract, "m.one", "m.zt")
+    op("c.jw", V, lambda: V.tensor_tensor(T.jw[:], T.pand[:], T.r16[:], A.add), "c.and", "i.r16")
 
     for t in range(3):
         ts("u0.%d" % t, T.ut0[:, t:512:4], zero, T.ub[:, t:t + 1], None, A.add, None, "ld.u", "m.zt")
     act("u0.3", T.ut0[:, 3:512:4], zero, AF.Identity, "ld.u", "m.zt", bias=T.ub[:, 3:4])
-    act("c.bias", T.bias[:], T.jw[:, 2:4], AF.Copy, "c.jw", scale=128.0, bias=64.0)
-    act("c.lo", T.lo[:], T.jw[:, 0:2], AF.Copy, "c.jw", scale=128.0)
-    act("c.hi", T.hi[:], T.jw[:, 0:2], AF.Copy, "c.jw", scale=128.0, bias=128.0)
-    act("c.ini", T.ini[:], T.jw[:, 0:2], AF.Copy, "c.jw", scale=16384.0, bias=16384.0)
+    act("c.ini", T.ini[:], T.jw[:, 0:2], AF.Copy, "c.jw", scale=-512.0, bias=-256.0)
+    act("c.top", T.top[:], T.jw[:, 0:2], AF.Copy, "c.jw", scale=-512.0, bias=32768.0 - 256.0)
     for t in range(4):
         act("u1.%d" % t, T.ut1[:, t:512:4], zero, AF.Identity, "ld.u", "m.zt", bias=T.ub[:, 4 + t:5 + t])
-    quant("q.u0", T.zc[:, 64:192], T.zs[:, 64:192], T.ut0[:], "u0.0", "u0.1", "u0.2", "u0.3")
 
     X = ("q.xA", "q.xB")
-    quant("q.xA", T.hold0c[:, 128:256], T.hold0s[:, 128:256], T.xt[:, 0:512], "ld.xA")
-    mm("t.sA", 0, 128, T.zc[:, 64:192], T.zs[:, 64:192], T.hold0c[:, 128:256], T.hold0s[:, 128:256], "q.u0", "q.xA")
-    quant("q.xB", T.hold0c[:, 256:384], T.hold0s[:, 256:384], T.xt[:, 512:1024], "ld.xB")
-    mm("t.sB", 1, 128, T.zc[:, 64:192], T.zs[:, 64:192], T.hold0c[:, 256:384], T.hold0s[:, 256:384], "q.u0", "q.xB")
-    ts("w.A", T.w0[:, 16:144], T.ps0[:, 0:128], 0.0, 64.0, A.is_lt, A.mult, "t.sA")
-    scan("f.A", T.f0[:, 0:128], T.w0[:, 16:144], T.w0[:, 15:143], 0.0, A.add, A.add, "w.A", "m.a0")
+    quant("q.xA", "hold0", 128, T.xt[:, 0:512], "ld.xA")
+    quant("q.u0", "z", 64, T.ut0[:], "u0.0", "u0.1", "u0.2", "u0.3")
+    mm("t.sA", 0, "z", 64, "hold0", 128, 128, "q.u0", "q.xA")
+    quant("q.xB", "hold0", 256, T.xt[:, 512:1024], "ld.xB")
+    mm("t.sB", 1, "z", 64, "hold0", 256, 128, "q.u0", "q.xB")
+    ts("w.A", T.w0[:, 16:144], T.ps0[:, 0:128], 0.0, 256.0, A.is_lt, A.mult, "t.sA")
     act("wb.A", T.wb0[:, 0:128], T.w0[:, 15:143], AF.Copy, "w.A", "m.a0", scale=1.015625)
-    ts("w.B", T.w0[:, 144:272], T.ps1[:, 0:128], 0.0, 64.0, A.is_lt, A.mult, "t.sB")
-    scan("f.0", T.f0[:, 128:257], T.w0[:, 144:273], T.w0[:, 143:272], T.f0[:, 127:128], A.add, A.add, "w.B", "f.A")
+    ts("w.B", T.w0[:, 144:272], T.ps1[:, 0:128], 0.0, 256.0, A.is_lt, A.mult, "t.sB")
+    tc("c.offd", T.offd[:], T.r32[:], *R32)
+    scan("f.0", T.f0[:, 0:257], T.w0[:, 16:273], T.w0[:, 15:272], T.ini[:, 0:1], A.add, A.add, "w.B", "w.A", "m.a0", "c.ini")
 
-    def lists(b):
-        f, acc, cl, su, off, junk = (T[k % b] for k in ("f%d", "acc%d", "clip%d", "sums%d", "off%d", "junk%d"))
-        n = "f.%d" % b
+    def lists(b, between=None):
+        f, h, acc, su, off, junk, w = (T[k % b] for k in ("f%d", "g%d", "acc%d", "sums%d", "off%d", "junk%d", "w%d"))
+        n, p = "f.%d" % b, 0 if b else 128
+        wd = ("w.1", "m.a1") if b else ("w.A", "w.B", "m.a0")
+        scan("g.%d" % b, h[:, 0:256], w[:, 16:272], w[:, 15:271], T.ini[:, 1:2], A.add, A.add, "c.ini", *wd)
+        act("wb.B%d" % b, T["wb%d" % b][:, p:256], w[:, 15 + p:271], AF.Copy, *wd, scale=1.015625)
         for m in range(2):
-            act("ps%d.%d" % (m, b), junk[:, 128 * m:128 * m + 112], f[:, 33:256:2], AF.Sign, n, "c.bias", scale=-1.0,
-                bias=T.bias[:, m:m + 1], accum_out=acc[:, m:m + 1])
-        for m in range(2):
-            ts("pm%d.%d" % (m, b), cl[:, 128 * m:128 * m + 128], f[:, 1:256:2], T.lo[:, m:m + 1], T.hi[:, m:m + 1], A.max, A.min,
-               n, "c.lo", "c.hi")
-        for m in range(2):
-            scan("pc%d.%d" % (m, b), su[:, 128 * m:128 * m + 128], zero, cl[:, 128 * m:128 * m + 128],
-                 T.ini[:, m:m + 1], A.add, A.subtract, "pm%d.%d" % (m, b), "c.ini")
-        p = 0 if b else 128
-        act("wb.B%d" % b, T["wb%d" % b][:, p:256], T["w%d" % b][:, 15 + p:271], AF.Copy, n, scale=1.015625)
+            act("ps%d.%d" % (m, b), junk[:, 128 * m:128 * m + 112], f[:, 33:256:2], AF.Sign, n, scale=-1.0,
+                bias=16384.0 + 8192.0 * m, accum_out=acc[:, m:m + 1])
+        scan("pc0.%d" % b, su[:, 0:256], f[:, 0:256], T.cap[:], 0.0, A.min, A.max, n, "c.cap")
+        scan("pc1.%d" % b, su[:, 272:512], h[:, 16:256], T.cap[:, 16:256], -16.0, A.min, A.max, "g.%d" % b, "c.cap")
+        if between:
+            between()
+        ts("ov.%d" % b, off[:, 0:2], su[:, 255:512:256], -1.0, 255.0, A.mult, A.min, "pc0.%d" % b, "pc1.%d" % b)
         ts("os.%d" % b, off[:, 2:4], acc[:, 0:2], 111.0, 144.0, A.min, A.add, "ps0.%d" % b, "ps1.%d" % b)
-        ts("ov.%d" % b, off[:, 0:2], su[:, 127:256:128], 0.015625, 255.0, A.mult, A.min, "pc0.%d" % b, "pc1.%d" % b)
 
-    def pick(name, oc, os, ic, is_, off, deps):
-        op(name + "c", V, lambda: V.tensor_copy(u32(oc), u32(ic).indirect(off)), *deps)
-        op(name + "s", S, lambda: S.activation(os, is_.indirect(off), AF.Copy), *deps)
+    def pick(name, o, a, n, i, p, q, off, *deps):
+        op(name + "c", V, lambda: V.tensor_copy(u32(T[o + "c"][:, a:a + n]), u32(T[i + "c"][:, p:q]).indirect(off)), *deps)
+        op(name + "s", S, lambda: S.activation(T[o + "s"][:, a:a + n], T[i + "s"][:, p:q].indirect(off), AF.Copy), *deps)
 
     def merge(b, i, p, q, *deps):
-        oc, os, c = (T.finc, T.fins, 0) if b else (T.hold1c, T.hold1s, 128)
-        pick("mg%d%d" % (b, i), oc[:, c + p:c + q], os[:, c + p:c + q], T["hold%dc" % b][:, 0:384], T["hold%ds" % b][:, 0:384],
-             T["offm%d" % b][:, 4 + p // 16:4 + q // 16], ("om.%d" % b, "q.n%d" % b) + deps)
+        pick("mg%d%d" % (b, i), "fin" if b else "hold1", p if b else 128 + p, q - p, "hold%d" % b, 0, 384,
+             T["offm%d" % b][:, 4 + p // 16:4 + q // 16], "om.%d" % b, "q.n%d" % b, *deps)
 
     def escan(b):
-        old = ("sc.0",) if b else ()
-        scan("e.%d" % b, T["e%d" % b][:], T["wb%d" % b][:], T["w%d" % b][:, 16:272], 64.0, A.add, A.subtract, "wb.B%d" % b,
+        scan("e.%d" % b, T["e%d" % b][:], T["wb%d" % b][:], T["w%d" % b][:, 16:272], 256.0, A.add, A.subtract, "wb.B%d" % b,
              "f.%d" % b, *(() if b else ("wb.A",)))
-        if not b:
-            tc("c.offd", T.offd[:], T.r32[:], *R32)
-        act("a2.%d" % b, T.d0[:, 33:36:2], T["sums%d" % b][:, 127:256:128], AF.Copy, "pc0.%d" % b, "pc1.%d" % b, *old,
-            scale=1 / (64 * UNIT))
-        act("a4.%d" % b, T.d0[:, 37:40:2], T["acc%d" % b][:, 0:2], AF.Copy, "ps0.%d" % b, "ps1.%d" % b, *old,
-            scale=1 / UNIT, bias=144 / UNIT)
+
+    def dup(b):
+        old = ("sc.0",) if b else ()
         act("dup.%d" % b, T["dup%d" % b][:], T["e%d" % b][:, 0:256].indirect(T.offd[:, 0:16]), AF.Copy, "e.%d" % b, "c.offd")
+        act("a2.%d" % b, T.d0[:, 49:54:3], T["sums%d" % b][:, 255:512:256], AF.Copy, "pc0.%d" % b, "pc1.%d" % b, "c.d0", *old,
+            scale=-1 / UNIT)
+        act("a4.%d" % b, T.d0[:, 55:60:3], T["acc%d" % b][:, 0:2], AF.Copy, "ps0.%d" % b, "ps1.%d" % b, *old,
+            scale=1 / UNIT, bias=144 / UNIT)
 
     def laid(b):
         op("tr.%d" % b, V, lambda: V.transpose(T.dtr[:, 0:256], T["dup%d" % b][:]), "dup.%d" % b, *(("sc.0",) if b else ()))
 
     def a16(b):
-        act("a16.%d" % b, T.d0[:, 1:32:2], T.dtr[:, 0:256:16], AF.Copy, "tr.%d" % b, scale=1 / UNIT, bias=NEW[b] / UNIT)
+        act("a16.%d" % b, T.d0[:, 1:48:3], T.dtr[:, 0:256:16], AF.Copy, "tr.%d" % b, scale=0.25 / UNIT, bias=NEW[b] / UNIT)
 
     def settle(b, part):
         if part == 0:
-            ts("th.%d" % b, T.th[:, b:b + 1], T["cnt%d" % b][:, 0:1], T["f%d" % b][:, 256:257], 8192.0, A.min, A.min,
-               "A.cnt%d" % b, "f.%d" % b)
+            ts("tm.%d" % b, T.tm[:, b:b + 1], T["f%d" % b][:, 256:257], T.top[:, 0:1], None, A.min, None, "f.%d" % b, "c.top")
         if part == 1:
-            ts("sel.%d" % b, T.d1[:, 0:40:2], T.dtr[:, 0:320:16], 128.0, T.th[:, b:b + 1], A.mult, A.is_ge, "th.%d" % b,
-               "tr.%d" % b, "c.idx")
+            ts("th.%d" % b, T.th[:, b:b + 1], T["cnt%d" % b][:, 0:1], T.tm[:, b:b + 1], T.ini[:, 0:1], A.min, A.subtract,
+               "tm.%d" % b, "A.cnt%d" % b)
         if part == 2:
-            scan("sc.%d" % b, T["res%d" % b][:], T.d0[:], T.d1[:], 0.0, A.add, A.min, "sel.%d" % b, "a16.%d" % b, "a2.%d" % b,
-                 "a4.%d" % b, "c.d0", "c.alt0", "c.alt1")
+            ts("sel.%d" % b, T.d1[:, 0:60:3], T.dtr[:, 0:320:16], 128.0, T.th[:, b:b + 1], A.mult, A.is_ge, "th.%d" % b,
+               "tr.%d" % b, "c.idx")
         if part == 3:
-            ts("om.%d" % b, T["offm%d" % b][:, 4:24], T["res%d" % b][:, 1:40:2], UNIT, None, A.mult, None, "sc.%d" % b)
+            scan("sc.%d" % b, T["res%d" % b][:], T.d0[:], T.d1[:], 0.0, A.add, A.min, "sel.%d" % b, "a16.%d" % b, "a2.%d" % b,
+                 "a4.%d" % b, "c.d0", "c.d1", "c.alt0", "c.alt1", *(("alt2",) if b else ()))
+        if part == 4:
+            ts("om.%d" % b, T["offm%d" % b][:, 4:24], T["res%d" % b][:, 1:60:3], UNIT, None, A.mult, None, "sc.%d" % b)
 
     def expert(b, i):
-        a, c = 512 * b + 128 * i, 2048 * b + 512 * i
-        quant("q.w%d%d" % (i, b), T.qwc[:, a:a + 128], T.qws[:, a:a + 128], T.wt[:, c:c + 512], "ld.w%d" % b)
+        quant("q.w%d%d" % (i, b), "qw", 512 * b + 128 * i, T.wt[:, 2048 * b + 512 * i:2048 * b + 512 * i + 512], "ld.w%d" % b)
 
-    def fresh(b):
-        h, hold, z, o = T.hz, "hold%d" % b, Z[b], 512 * b
+    def fresh(b, between=None):
+        o = 512 - 512 * b
         for i in range(4):
-            a = 512 * b + 128 * i
-            mm("R%d.%d" % (i, b), 4 + i, 128, T.qwc[:, a:a + 128], T.qws[:, a:a + 128], T.zc[:, z:z + 128], T.zs[:, z:z + 128],
+            mm("R%d.%d" % (i, b), 4 + i, "qw", 512 * b + 128 * i, "z", Z[b], 128,
                "q.w%d%d" % (i, b), "q.u0", "A.cod%d" % b, "A.scl%d" % b, *(("K%d.0" % i,) if b else ()))
         for i in range(4):
             r = T["ps%d" % (4 + i)][:, NEW[b]:NEW[b] + 64]
-            if i == 3:
-                ts("K%d.%d" % (i, b), h[:, o + i:o + 256:4], r, 0.0625, None, A.mult, None, "R%d.%d" % (i, b))
+            if i >= 2:
+                ts("K%d.%d" % (i, b), T.hz[:, o + i:o + 256:4], r, 0.0625, None, A.mult, None, "R%d.%d" % (i, b))
             else:
-                act("K%d.%d" % (i, b), h[:, o + i:o + 256:4], r, AF.Copy, "R%d.%d" % (i, b), scale=0.0625)
-        quant("q.n%d" % b, T[hold + "c"][:, 0:128], T[hold + "s"][:, 0:128], h[:, 256 * b:256 * b + 512],
-              *["K%d.%d" % (i, b) for i in range(4)], "m.zt")
+                act("K%d.%d" % (i, b), T.hz[:, o + i:o + 256:4], r, AF.Copy, "R%d.%d" % (i, b), scale=0.0625)
+        if between:
+            between()
+        quant("q.n%d" % b, "hold%d" % b, 0, T.hz[:, 256 - 256 * b:768 - 256 * b], *["K%d.%d" % (i, b) for i in range(4)], "m.zt")
+
+    def swap(b, to, *deps):
+        a = Z[b] + NEW[b]
+        pick("pk%d" % b, "snd%d" % b, 0, 64, "hold%d" % b, 128, 384, T["off%d" % b][:, 0:4], "ov.%d" % b, "os.%d" % b, *deps)
+        send("g.cod%d" % b, to, u8(T.zc[:, a:a + 64]), u8(T["snd%dc" % b][:, 0:64]), "rcod%d" % b, "pk%dc" % b)
+        send("g.scl%d" % b, to, T.zs[:, a:a + 64], T["snd%ds" % b][:, 0:64], "rscl%d" % b, "pk%ds" % b)
 
     send("g.cnt0", mate0, T.cnt0[:, 0:1], T.f0[:, 256:257], "rcnt0", "f.0", lsem="lcnt")
     lists(0)
-    pick("pk0", T.snd0c[:], T.snd0s[:], T.hold0c[:, 128:384], T.hold0s[:, 128:384], T.off0[:, 0:4], ("ov.0", "os.0") + X)
-    send("g.cod0", mate0, u8(T.zc[:, 0:64]), u8(T.snd0c[:, 0:64]), "rcod0", "pk0c")
-    send("g.scl0", mate0, T.zs[:, 0:64], T.snd0s[:, 0:64], "rscl0", "pk0s")
+    escan(0)
+    swap(0, mate0, *X)
     send("g.lst", mate0, T.offm0[:, 24:28], T.off0[:, 0:4], "rlst", "ov.0", "os.0")
     op("g.go", g, lambda: g.sem_inc(T.sem["go"], 1))
     move("ld.w1", Y, T.wt[:, 2048:4096], T.w[:, 2048:4096], "E.go", "L.cnt")
-    move("ld.v", Y, T.vt[:], T.v[:])
-    iota("i.idw0", T.idw0[:], [[1, 384]], 256 * rank - 128, 0, True, *R32)
-    iota("i.pid", T.pid[:, 0:256], [[1, 256]], 256 * mate1, 0, True)
-    iota("i.idw1", T.idw1[:, 0:64], [[1, 64]], 0, 0, True)
+    iota("i.idw", T.idw[:], [[1, 384]], 256 * rank - 128, *R32)
+    iota("i.pid", T.pid[:, 0:256], [[1, 256]], 256 * mate1)
 
-    act("c.alt1", T.d1[:, 1:32:2], T.jw[:], AF.Copy, "c.jw", scale=1 / UNIT, bias=128 / UNIT)
-    escan(0)
-    act("c.alt0", T.d1[:, 33:40:2], T.jw[:, 0:4], AF.Copy, "c.jw", scale=1 / UNIT, bias=264 / UNIT)
-    act("c.idx", T.dtr[:, 256:320:16], T.jw[:, 0:4], AF.Copy, "c.jw")
-    quant("q.u1", T.qu1c[:], T.qu1s[:], T.ut1[:], "u1.0", "u1.1", "u1.2", "u1.3")
-    mm("t.s1", 2, 256, T.qu1c[:], T.qu1s[:], T.hold0c[:, 128:384], T.hold0s[:, 128:384], "q.u1", *X)
+    act("c.alt1", T.d1[:, 1:48:3], T.jw[:], AF.Copy, "c.jw", scale=1 / UNIT, bias=128 / UNIT)
+    dup(0)
+    act("c.alt0", T.d1[:, 49:60:3], T.jw[:, 0:4], AF.Copy, "c.jw", scale=1 / UNIT, bias=264 / UNIT)
+    act("c.idx", T.dtr[:, 256:320:16], T.jw[:, 0:4], AF.Copy, "c.jw", scale=4.0)
+    quant("q.u1", "qu1", 0, T.ut1[:], "u1.0", "u1.1", "u1.2", "u1.3")
+    mm("t.s1", 2, "qu1", 0, "hold0", 128, 256, "q.u1", *X)
     act("sg.1", T.sig[:], T.ps2[:, 0:256], AF.Sign, "t.s1", scale=-1.0)
     for i in range(4):
         expert(0, i)
+    quant("q.v", "qv", 0, T.vt[:], "ld.v")
+    settle(0, 0)
     laid(0)
     a16(0)
-    act("w.1x", T.w1[:, 16:272], T.sig[:], AF.Relu, "sg.1", scale=64.0)
-    for part in range(4):
+    act("w.1x", T.w1[:, 16:272], T.sig[:], AF.Relu, "sg.1", scale=256.0)
+    for part in (1, 2, 3):
         settle(0, part)
-    send("g.pof", mate1, T.pof[:], T.offm0[:, 20:28], "rpof", "om.0", "A.lst")
 
-    fresh(0)
-    mm("t.sN", 0, 128, T.qu1c[:], T.qu1s[:], T.hold0c[:, 0:128], T.hold0s[:, 0:128], "q.n0", "w.A")
-    merge(0, 0, 0, 160, *X)
-    ts("w.N", T.wn[:], T.ps0[:, 0:64], 0.0, 64.0, A.is_lt, A.mult, "t.sN")
-    merge(0, 1, 160, 192, *X)
+    fresh(0, lambda: settle(0, 4))
+    send("g.pof", mate1, T.pof[:], T.offm0[:, 20:28], "rpof", "om.0", "A.lst")
+    mm("t.sN", 0, "qu1", 0, "hold0", 0, 128, "q.n0", "w.A")
+    merge(0, 0, 0, 128, *X)
+    ts("w.N", T.wn[:], T.ps0[:, 64:128], 0.0, 256.0, A.is_lt, A.mult, "t.sN")
+    merge(0, 1, 128, 160, *X)
     tc("w.1", T.w1[:, 16:352].indirect(T.offm0[:, 20:24]), T.wn[:], "w.N", "w.1x", "om.0")
-    merge(0, 2, 192, 224, *X)
-    scan("f.1", T.f1[:, 0:257], T.w1[:, 16:273], T.w1[:, 15:272], 0.0, A.add, A.add, "w.1", "m.a1")
+    merge(0, 2, 160, 192, *X)
+    scan("f.1", T.f1[:, 0:257], T.w1[:, 16:273], T.w1[:, 15:272], T.ini[:, 0:1], A.add, A.add, "w.1", "m.a1")
 
     send("g.cnt1", mate1, T.cnt1[:, 0:1], T.f1[:, 256:257], "rcnt1", "f.1")
-    merge(0, 3, 224, 256, *X)
-    act("id.a", T.idw0[:, 0:64], T.idw0[:, 128:384].indirect(T.offm0[:, 24:28]), AF.Copy, "A.lst", "i.idw0",
+    act("alt2", T.d1[:, 2:48:3], T.res0[:, 1:48:3], AF.Copy, "sc.0")
+    act("id.a", T.idw[:, 64:128], T.idw[:, 128:384].indirect(T.offm0[:, 24:28]), AF.Copy, "A.lst", "i.idw",
         bias=float(256 * (mate0 - rank)))
-    lists(1)
-    M = tuple("mg0%d%s" % (i, k) for i in range(4) for k in "cs")
-    pick("pk1", T.snd1c[:], T.snd1s[:], T.hold1c[:, 128:384], T.hold1s[:, 128:384], T.off1[:, 0:4], ("ov.1", "os.1") + M)
-    send("g.cod1", mate1, u8(T.zc[:, 192:256]), u8(T.snd1c[:, 0:64]), "rcod1", "pk1c")
-    send("g.scl1", mate1, T.zs[:, 192:256], T.snd1s[:, 0:64], "rscl1", "pk1s")
-    send("g.lst1", mate1, T.lin1[:], T.off1[:, 0:4], "rlst1", "ov.1", "os.1")
+    lists(1, lambda: merge(0, 3, 192, 256, *X))
     escan(1)
-    quant("q.v", T.qvc[:], T.qvs[:], T.vt[:], "ld.v")
-    mm("t.y", 3, 256, T.qvc[:], T.qvs[:], T.hold1c[:, 128:384], T.hold1s[:, 128:384], "q.v", *M)
-    for i in range(4):
+    M = tuple("mg0%d%s" % (i, k) for i in range(4) for k in "cs")
+    swap(1, mate1, *M)
+    send("g.lst1", mate1, T.lin1[:], T.off1[:, 0:4], "rlst1", "ov.1", "os.1")
+    dup(1)
+    mm("t.y", 3, "qv", 0, "hold1", 128, 256, "q.v", *M)
+    for i in range(3):
         expert(1, i)
     settle(1, 0)
+    expert(1, 3)
+    settle(1, 1)
     laid(1)
-    act("id.p", T.ptmp[:], T.idw0[:, 128:384].indirect(T.pof[:, 4:8]), AF.Copy, "A.pof", "i.idw0", bias=float(256 * (far - rank)))
+    act("id.p", T.ptmp[:], T.idw[:, 128:384].indirect(T.pof[:, 4:8]), AF.Copy, "A.pof", "i.idw", bias=float(256 * (far - rank)))
     act("y.m", T.yrow[:, 0:256], T.ps3[:, 0:256], AF.Copy, "t.y")
     a16(1)
-    settle(1, 1)
-    tc("id.q", T.pid[:, 0:336].indirect(T.pof[:, 0:4]), T.ptmp[:], "A.pof", "id.p", "i.pid")
     settle(1, 2)
+    tc("id.q", T.pid[:, 0:336].indirect(T.pof[:, 0:4]), T.ptmp[:], "A.pof", "id.p", "i.pid")
     settle(1, 3)
-    act("id.m", T.idw1[:, 128:384], T.idw0[:].indirect(T.offm0[:, 4:20]), AF.Copy, "id.a", "i.idw0", "om.0")
+    settle(1, 4)
+    ts("om.i", T.offi[:], T.res1[:, 2:48:3], UNIT, None, A.mult, None, "sc.1")
+    act("ks", T.ksb[:], T.th[:], AF.Copy, "th.0", "th.1", scale=1 / 512)
     fresh(1)
-    act("id.n", T.idw1[:, 64:128], T.pid[:, 0:256].indirect(T.lin1[:, 0:4]), AF.Copy, "id.q", "A.lst1")
-    act("ks", T.ksb[:], T.th[:], AF.Copy, "th.0", "th.1", scale=0.0078125)
-    act("id.f", T.idf[:], T.idw1[:].indirect(T.offm1[:, 4:20]), AF.Copy, "id.m", "id.n", "i.idw1", "om.1")
-    mm("t.yn", 1, 128, T.qvc[:], T.qvs[:], T.hold1c[:, 0:128], T.hold1s[:, 0:128], "q.n1", "q.v", "w.B")
-    act("y.n", T.yn[:], T.ps1[:, 64:128], AF.Copy, "t.yn")
+    act("id.n", T.idw[:, 0:64], T.pid[:, 0:256].indirect(T.lin1[:, 0:4]), AF.Copy, "id.q", "A.lst1", "i.idw")
+    act("id.f", T.idf[:], T.idw[:].indirect(T.offi[:, 0:16]), AF.Copy, "id.a", "id.n", "om.i")
+    mm("t.yn", 1, "qv", 0, "hold1", 0, 128, "q.n1", "q.v", "w.B")
     merge(1, 0, 0, 256, *M)
+    tc("y.n", T.yn[:], T.ps1[:, 0:64], "t.yn")
     tc("y.s", T.yrow[:, 0:336].indirect(T.offm1[:, 20:24]), T.yn[:], "y.n", "y.m", "om.1")
 
     move("st.k", Y, T.ks[0:1, 0:2], T.ksb[0:1, 0:2], "ks")

from concourse.mybir import dt, AluOpType as A, ActivationFunctionType as AF

F8, BF, U16 = "float8_e4m3fn_x4", "bfloat16", "uint16"


def _sb(n, t="float32"):
    return ("sbuf", [128, n], t)


SCRATCH = {"pidx": _sb(16, "int32"), "pand": _sb(16, "int32"), "r32": _sb(16, "int32")}
for _n, _k in dict(pof=8, lin1=4, offd=16, offi=16, off0=4, off1=4, offm0=28, offm1=28).items():
    SCRATCH[_n] = _sb(_k, U16)
for _n, _k in dict(cnt0=1, cnt1=1, ub=8, xt=1024, wt=4096, vt=512, ut0=512, ut1=512, hz=768, w0=288, w1=352, wn=64, sig=256,
                   dtr=320, cap=256).items():
    SCRATCH[_n] = _sb(_k, BF)
for _n, _k in dict(qu1=128, qw=1024, qv=128, hold0=384, hold1=384, fin=256, snd0=64, snd1=64, z=256).items():
    SCRATCH[_n + "c"], SCRATCH[_n + "s"] = _sb(_k, F8), _sb(_k, "uint8")
for _n, _k in dict(r16=16, jw=16, top=2, ini=2, th=2, tm=2, ksb=2, pid=336, d0=60, d1=60, ptmp=64, idw=384, idf=256,
                   yrow=336, yn=64, acc0=2, acc1=2, res0=60, res1=60).items():
    SCRATCH[_n] = _sb(_k)
for _b in "01":
    for _n, _k in dict(f=272, g=256, junk=256, sums=512, wb=256, e=256, dup=256).items():
        SCRATCH[_n + _b] = _sb(_k, BF)
for _b in range(8):
    SCRATCH["ps%d" % _b] = ("psum", [128, 512], "float32")

REMOTE = ["rcnt0", "rcod0", "rscl0", "rlst", "rpof", "rcnt1", "rlst1", "rcod1", "rscl1", "lall", "lcnt", "go"]
POOL = 80
SEMAPHORES = REMOTE + ["s%d" % _i for _i in range(POOL)]
Z = (128, 0)
NEW = (64, 0)
UNIT = 1024.0


def rank_program(g, core, T, topo):
    rank = T.rank_of(core)
    if rank is None:
        return
    cores = T.cores
    mate0, mate1, far = rank ^ 1, rank ^ 2, rank ^ 3
    V, S, P, Y = g.vector, g.scalar, g.tensor, g.sync
    ops, local = [], {"lall": 0, "lcnt": 0}

    def op(name, queue, fn, *deps, dma=False):
        ops.append((name, queue, fn, deps, dma))

    def eng(a, b):
        return len(topo.engines(cores[a], cores[b]))
    arrive = {"A.lst": ("rlst", eng(mate0, rank)), "A.pof": ("rpof", eng(mate1, rank)), "A.lst1": ("rlst1", eng(mate1, rank)),
              "E.go": ("go", 1), "L.cnt": ("lcnt", eng(rank, mate0))}
    for b, m in ((0, mate0), (1, mate1)):
        for kind in ("cnt", "cod", "scl"):
            arrive["A.%s%d" % (kind, b)] = ("r%s%d" % (kind, b), eng(m, rank))

    def send(name, to, dst, src, sem, *deps, lsem="lall"):
        rid, pid, _ = topo.addr(cores[to])
        local[lsem] += eng(rank, to)
        op(name, g, lambda: g.remote_dma(out_ap=dst, in_ap=src, remote_sem=T.sem[sem], local_sem=T.sem[lsem], pid=pid,
                                         routing_id=rid, dma_engine_mask=topo.mask(core, cores[to])), *deps)

    def u8(v):
        return v.bitcast(dt.uint8)

    def u32(v):
        return v.bitcast(dt.uint32)

    def mm(name, bank, q, a, x, p, n, *deps):
        op(name, P, lambda: P.matmul_mx(T["ps%d" % bank][:, 0:n], T[q + "c"][:, a:a + 128], T[q + "s"][:, a:a + 128],
                                        T[x + "c"][:, p:p + n], T[x + "s"][:, p:p + n], True, True), *deps)

    def ts(name, out, in0, s1, s2, o0, o1, *deps):
        if o1 is None:
            op(name, V, lambda: V.tensor_scalar(out, in0, s1, None, o0), *deps)
        else:
            op(name, V, lambda: V.tensor_scalar(out, in0, s1, s2, o0, o1), *deps)

    def tc(name, out, in_, *deps):
        op(name, V, lambda: V.tensor_copy(out, in_), *deps)

    def scan(name, out, a, b, init, o0, o1, *deps):
        op(name, V, lambda: V.tensor_tensor_scan(out, a, b, init, o0, o1), *deps)

    def act(name, out, in_, fn, *deps, **kw):
        op(name, S, lambda: S.activation(out, in_, fn, **kw), *deps)

    def quant(name, q, a, t, *deps):
        op(name, V, lambda: V.quantize_mx(T[q + "c"][:, a:a + 128], T[q + "s"][:, a:a + 128], t), *deps)

    def move(name, q, out, in_, *deps):
        op(name, q, lambda: q.dma_start(out, in_), *deps, dma=True)

    def iota(name, out, pattern, base, *deps):
        op(name, g, lambda: g.iota(out, pattern, base, 0, allow_small_or_imprecise_dtypes=True), *deps)

    def iotp(name, out, pattern, *deps):
        op(name, g, lambda: g.iota(out, pattern, 0, 1), *deps)

    zero = T.hz[:, 256:384]

    move("ld.u", S, T.ub[:, 0:8], T.u[:, 0:8])
    move("ld.xA", Y, T.xt[:, 0:512], T.x[:, 0:512])
    move("ld.xB", Y, T.xt[:, 512:1024], T.x[:, 512:1024])
    move("ld.w0", Y, T.wt[:, 0:2048], T.w[:, 0:2048])
    move("ld.v", Y, T.vt[:], T.v[:])

    iotp("i.p", T.pidx[:], [[0, 16]])
    iota("i.r16", T.r16[:], [[16, 16]], 0)
    iota("m.a0", T.w0[:, 15:273:257], [[0, 2]], 0)
    iota("m.a1", T.w1[:, 15:273:257], [[0, 2]], 0)
    iota("c.d0", T.d0[:], [[0, 20], [-2, 3]], 4)
    iota("c.d1", T.d1[:, 2:60:3], [[0, 20]], 1)
    for a in range(4):
        iotp("i.r32%d" % a, T.r32[32 * a:32 * a + 32, :], [[32, 8], [0, 2]], "i.p", "i.r16", "m.a0", "m.a1", "c.d0", "c.d1")
    R32 = tuple("i.r32%d" % a for a in range(4))
    op("m.zt", V, lambda: V.memset(T.hz[:, 256:512], 0.0))
    op("m.one", V, lambda: V.memset(T.junk1[:], 1.0))
    ts("c.and", T.pand[:], T.pidx[:], 15, None, A.bitwise_and, None, "i.p")
    scan("c.cap", T.cap[:], T.hz[:, 256:512], T.junk1[:], 0.0, A.add, A.subtract, "m.one", "m.zt")
    op("c.jw", V, lambda: V.tensor_tensor(T.jw[:], T.pand[:], T.r16[:], A.add), "c.and", "i.r16")

    for t in range(3):
        ts("u0.%d" % t, T.ut0[:, t:512:4], zero, T.ub[:, t:t + 1], None, A.add, None, "ld.u", "m.zt")
    act("u0.3", T.ut0[:, 3:512:4], zero, AF.Identity, "ld.u", "m.zt", bias=T.ub[:, 3:4])
    act("c.ini", T.ini[:], T.jw[:, 0:2], AF.Copy, "c.jw", scale=-512.0, bias=-256.0)
    act("c.top", T.top[:], T.jw[:, 0:2], AF.Copy, "c.jw", scale=-512.0, bias=32768.0 - 256.0)
    for t in range(4):
        act("u1.%d" % t, T.ut1[:, t:512:4], zero, AF.Identity, "ld.u", "m.zt", bias=T.ub[:, 4 + t:5 + t])

    X = ("q.xA", "q.xB")
    quant("q.xA", "hold0", 128, T.xt[:, 0:512], "ld.xA")
    quant("q.u0", "z", 64, T.ut0[:], "u0.0", "u0.1", "u0.2", "u0.3")
    mm("t.sA", 0, "z", 64, "hold0", 128, 128, "q.u0", "q.xA")
    quant("q.xB", "hold0", 256, T.xt[:, 512:1024], "ld.xB")
    mm("t.sB", 1, "z", 64, "hold0", 256, 128, "q.u0", "q.xB")
    ts("w.A", T.w0[:, 16:144], T.ps0[:, 0:128], 0.0, 256.0, A.is_lt, A.mult, "t.sA")
    act("wb.A", T.wb0[:, 0:128], T.w0[:, 15:143], AF.Copy, "w.A", "m.a0", scale=1.015625)
    ts("w.B", T.w0[:, 144:272], T.ps1[:, 0:128], 0.0, 256.0, A.is_lt, A.mult, "t.sB")
    tc("c.offd", T.offd[:], T.r32[:], *R32)
    scan("f.0", T.f0[:, 0:257], T.w0[:, 16:273], T.w0[:, 15:272], T.ini[:, 0:1], A.add, A.add, "w.B", "w.A", "m.a0", "c.ini")

    def lists(b, between=None):
        f, h, acc, su, off, junk, w = (T[k % b] for k in ("f%d", "g%d", "acc%d", "sums%d", "off%d", "junk%d", "w%d"))
        n, p = "f.%d" % b, 0 if b else 128
        wd = ("w.1", "m.a1") if b else ("w.A", "w.B", "m.a0")
        scan("g.%d" % b, h[:, 0:256], w[:, 16:272], w[:, 15:271], T.ini[:, 1:2], A.add, A.add, "c.ini", *wd)
        act("wb.B%d" % b, T["wb%d" % b][:, p:256], w[:, 15 + p:271], AF.Copy, *wd, scale=1.015625)
        for m in range(2):
            act("ps%d.%d" % (m, b), junk[:, 128 * m:128 * m + 112], f[:, 33:256:2], AF.Sign, n, scale=-1.0,
                bias=16384.0 + 8192.0 * m, accum_out=acc[:, m:m + 1])
        scan("pc0.%d" % b, su[:, 0:256], f[:, 0:256], T.cap[:], 0.0, A.min, A.max, n, "c.cap")
        scan("pc1.%d" % b, su[:, 272:512], h[:, 16:256], T.cap[:, 16:256], -16.0, A.min, A.max, "g.%d" % b, "c.cap")
        if between:
            between()
        ts("ov.%d" % b, off[:, 0:2], su[:, 255:512:256], -1.0, 255.0, A.mult, A.min, "pc0.%d" % b, "pc1.%d" % b)
        ts("os.%d" % b, off[:, 2:4], acc[:, 0:2], 111.0, 144.0, A.min, A.add, "ps0.%d" % b, "ps1.%d" % b)

    def pick(name, o, a, n, i, p, q, off, *deps):
        op(name + "c", V, lambda: V.tensor_copy(u32(T[o + "c"][:, a:a + n]), u32(T[i + "c"][:, p:q]).indirect(off)), *deps)
        op(name + "s", S, lambda: S.activation(T[o + "s"][:, a:a + n], T[i + "s"][:, p:q].indirect(off), AF.Copy), *deps)

    def merge(b, i, p, q, *deps):
        pick("mg%d%d" % (b, i), "fin" if b else "hold1", p if b else 128 + p, q - p, "hold%d" % b, 0, 384,
             T["offm%d" % b][:, 4 + p // 16:4 + q // 16], "om.%d" % b, "q.n%d" % b, *deps)

    def escan(b):
        scan("e.%d" % b, T["e%d" % b][:], T["wb%d" % b][:], T["w%d" % b][:, 16:272], 256.0, A.add, A.subtract, "wb.B%d" % b,
             "f.%d" % b, *(() if b else ("wb.A",)))

    def dup(b):
        old = ("sc.0",) if b else ()
        act("dup.%d" % b, T["dup%d" % b][:], T["e%d" % b][:, 0:256].indirect(T.offd[:, 0:16]), AF.Copy, "e.%d" % b, "c.offd")
        act("a2.%d" % b, T.d0[:, 49:54:3], T["sums%d" % b][:, 255:512:256], AF.Copy, "pc0.%d" % b, "pc1.%d" % b, "c.d0", *old,
            scale=-1 / UNIT)
        act("a4.%d" % b, T.d0[:, 55:60:3], T["acc%d" % b][:, 0:2], AF.Copy, "ps0.%d" % b, "ps1.%d" % b, *old,
            scale=1 / UNIT, bias=144 / UNIT)

    def laid(b):
        op("tr.%d" % b, V, lambda: V.transpose(T.dtr[:, 0:256], T["dup%d" % b][:]), "dup.%d" % b, *(("sc.0",) if b else ()))

    def a16(b):
        act("a16.%d" % b, T.d0[:, 1:48:3], T.dtr[:, 0:256:16], AF.Copy, "tr.%d" % b, scale=0.25 / UNIT, bias=NEW[b] / UNIT)

    def settle(b, part):
        if part == 0:
            ts("tm.%d" % b, T.tm[:, b:b + 1], T["f%d" % b][:, 256:257], T.top[:, 0:1], None, A.min, None, "f.%d" % b, "c.top")
        if part == 1:
            ts("th.%d" % b, T.th[:, b:b + 1], T["cnt%d" % b][:, 0:1], T.tm[:, b:b + 1], T.ini[:, 0:1], A.min, A.subtract,
               "tm.%d" % b, "A.cnt%d" % b)
        if part == 2:
            ts("sel.%d" % b, T.d1[:, 0:60:3], T.dtr[:, 0:320:16], 128.0, T.th[:, b:b + 1], A.mult, A.is_ge, "th.%d" % b,
               "tr.%d" % b, "c.idx")
        if part == 3:
            scan("sc.%d" % b, T["res%d" % b][:], T.d0[:], T.d1[:], 0.0, A.add, A.min, "sel.%d" % b, "a16.%d" % b, "a2.%d" % b,
                 "a4.%d" % b, "c.d0", "c.d1", "c.alt0", "c.alt1", *(("alt2",) if b else ()))
        if part == 4:
            ts("om.%d" % b, T["offm%d" % b][:, 4:24], T["res%d" % b][:, 1:60:3], UNIT, None, A.mult, None, "sc.%d" % b)

    def expert(b, i):
        quant("q.w%d%d" % (i, b), "qw", 512 * b + 128 * i, T.wt[:, 2048 * b + 512 * i:2048 * b + 512 * i + 512], "ld.w%d" % b)

    def fresh(b, between=None):
        o = 512 - 512 * b
        for i in range(4):
            mm("R%d.%d" % (i, b), 4 + i, "qw", 512 * b + 128 * i, "z", Z[b], 128,
               "q.w%d%d" % (i, b), "q.u0", "A.cod%d" % b, "A.scl%d" % b, *(("K%d.0" % i,) if b else ()))
        for i in range(4):
            r = T["ps%d" % (4 + i)][:, NEW[b]:NEW[b] + 64]
            if i >= 2:
                ts("K%d.%d" % (i, b), T.hz[:, o + i:o + 256:4], r, 0.0625, None, A.mult, None, "R%d.%d" % (i, b))
            else:
                act("K%d.%d" % (i, b), T.hz[:, o + i:o + 256:4], r, AF.Copy, "R%d.%d" % (i, b), scale=0.0625)
        if between:
            between()
        quant("q.n%d" % b, "hold%d" % b, 0, T.hz[:, 256 - 256 * b:768 - 256 * b], *["K%d.%d" % (i, b) for i in range(4)], "m.zt")

    def swap(b, to, *deps):
        a = Z[b] + NEW[b]
        pick("pk%d" % b, "snd%d" % b, 0, 64, "hold%d" % b, 128, 384, T["off%d" % b][:, 0:4], "ov.%d" % b, "os.%d" % b, *deps)
        send("g.cod%d" % b, to, u8(T.zc[:, a:a + 64]), u8(T["snd%dc" % b][:, 0:64]), "rcod%d" % b, "pk%dc" % b)
        send("g.scl%d" % b, to, T.zs[:, a:a + 64], T["snd%ds" % b][:, 0:64], "rscl%d" % b, "pk%ds" % b)

    send("g.cnt0", mate0, T.cnt0[:, 0:1], T.f0[:, 256:257], "rcnt0", "f.0", lsem="lcnt")
    lists(0)
    escan(0)
    swap(0, mate0, *X)
    send("g.lst", mate0, T.offm0[:, 24:28], T.off0[:, 0:4], "rlst", "ov.0", "os.0")
    op("g.go", g, lambda: g.sem_inc(T.sem["go"], 1))
    move("ld.w1", Y, T.wt[:, 2048:4096], T.w[:, 2048:4096], "E.go", "L.cnt")
    iota("i.idw", T.idw[:], [[1, 384]], 256 * rank - 128, *R32)
    iota("i.pid", T.pid[:, 0:256], [[1, 256]], 256 * mate1)

    act("c.alt1", T.d1[:, 1:48:3], T.jw[:], AF.Copy, "c.jw", scale=1 / UNIT, bias=128 / UNIT)
    dup(0)
    act("c.alt0", T.d1[:, 49:60:3], T.jw[:, 0:4], AF.Copy, "c.jw", scale=1 / UNIT, bias=264 / UNIT)
    act("c.idx", T.dtr[:, 256:320:16], T.jw[:, 0:4], AF.Copy, "c.jw", scale=4.0)
    quant("q.u1", "qu1", 0, T.ut1[:], "u1.0", "u1.1", "u1.2", "u1.3")
    mm("t.s1", 2, "qu1", 0, "hold0", 128, 256, "q.u1", *X)
    act("sg.1", T.sig[:], T.ps2[:, 0:256], AF.Sign, "t.s1", scale=-1.0)
    for i in range(4):
        expert(0, i)
    quant("q.v", "qv", 0, T.vt[:], "ld.v")
    settle(0, 0)
    laid(0)
    a16(0)
    act("w.1x", T.w1[:, 16:272], T.sig[:], AF.Relu, "sg.1", scale=256.0)
    for part in (1, 2, 3):
        settle(0, part)

    fresh(0, lambda: settle(0, 4))
    send("g.pof", mate1, T.pof[:], T.offm0[:, 20:28], "rpof", "om.0", "A.lst")
    mm("t.sN", 0, "qu1", 0, "hold0", 0, 128, "q.n0", "w.A")
    merge(0, 0, 0, 128, *X)
    ts("w.N", T.wn[:], T.ps0[:, 64:128], 0.0, 256.0, A.is_lt, A.mult, "t.sN")
    merge(0, 1, 128, 160, *X)
    tc("w.1", T.w1[:, 16:352].indirect(T.offm0[:, 20:24]), T.wn[:], "w.N", "w.1x", "om.0")
    merge(0, 2, 160, 192, *X)
    scan("f.1", T.f1[:, 0:257], T.w1[:, 16:273], T.w1[:, 15:272], T.ini[:, 0:1], A.add, A.add, "w.1", "m.a1")

    send("g.cnt1", mate1, T.cnt1[:, 0:1], T.f1[:, 256:257], "rcnt1", "f.1")
    act("alt2", T.d1[:, 2:48:3], T.res0[:, 1:48:3], AF.Copy, "sc.0")
    act("id.a", T.idw[:, 64:128], T.idw[:, 128:384].indirect(T.offm0[:, 24:28]), AF.Copy, "A.lst", "i.idw",
        bias=float(256 * (mate0 - rank)))
    lists(1, lambda: merge(0, 3, 192, 256, *X))
    escan(1)
    M = tuple("mg0%d%s" % (i, k) for i in range(4) for k in "cs")
    swap(1, mate1, *M)
    send("g.lst1", mate1, T.lin1[:], T.off1[:, 0:4], "rlst1", "ov.1", "os.1")
    dup(1)
    mm("t.y", 3, "qv", 0, "hold1", 128, 256, "q.v", *M)
    for i in range(3):
        expert(1, i)
    settle(1, 0)
    expert(1, 3)
    settle(1, 1)
    laid(1)
    act("id.p", T.ptmp[:], T.idw[:, 128:384].indirect(T.pof[:, 4:8]), AF.Copy, "A.pof", "i.idw", bias=float(256 * (far - rank)))
    act("y.m", T.yrow[:, 0:256], T.ps3[:, 0:256], AF.Copy, "t.y")
    a16(1)
    settle(1, 2)
    tc("id.q", T.pid[:, 0:336].indirect(T.pof[:, 0:4]), T.ptmp[:], "A.pof", "id.p", "i.pid")
    settle(1, 3)
    settle(1, 4)
    ts("om.i", T.offi[:], T.res1[:, 2:48:3], UNIT, None, A.mult, None, "sc.1")
    act("ks", T.ksb[:], T.th[:], AF.Copy, "th.0", "th.1", scale=1 / 512)
    fresh(1)
    act("id.n", T.idw[:, 0:64], T.pid[:, 0:256].indirect(T.lin1[:, 0:4]), AF.Copy, "id.q", "A.lst1", "i.idw")
    act("id.f", T.idf[:], T.idw[:].indirect(T.offi[:, 0:16]), AF.Copy, "id.a", "id.n", "om.i")
    mm("t.yn", 1, "qv", 0, "hold1", 0, 128, "q.n1", "q.v", "w.B")
    merge(1, 0, 0, 256, *M)
    tc("y.n", T.yn[:], T.ps1[:, 0:64], "t.yn")
    tc("y.s", T.yrow[:, 0:336].indirect(T.offm1[:, 20:24]), T.yn[:], "y.n", "y.m", "om.1")

    move("st.k", Y, T.ks[0:1, 0:2], T.ksb[0:1, 0:2], "ks")
    move("st.i", Y, T.ids[0:1, :], T.idf[0:1, :], "id.f")
    move("st.c", Y, T.oc[:, :], u8(T.finc[:, 0:256]), "mg10c")
    move("st.y", Y, T.y[:, :], T.yrow[:, 0:256], "y.s")
    for k in range(4):
        move("st.s%d" % k, S if k < 3 else Y, T.osc[4 * k:4 * k + 4, 0:256], T.fins[32 * k:32 * k + 4, 0:256], "mg10s")
    op("end", Y, None, "st.k", "st.i", "st.c", "st.y", "st.s0", "st.s1", "st.s2", "st.s3")

    qs = (g, V, S, P, Y)
    known, seen, waits, needed = [set() for _ in qs], {}, [], set()

    def number(q):
        return [i for i in range(5) if qs[i] is q][0]
    for name, q, fn, deps, dma in ops:
        i, w = number(q), []
        for dep in deps:
            if dep not in known[i]:
                w.append(dep)
                known[i] |= {dep} | seen.get(dep, set())
                needed.add(dep)
        seen[name] = set(known[i])
        waits.append(w)
    pool, mark = [], {e: arrive[e] for e in arrive}
    for name, q, fn, deps, dma in ops:
        if name in needed:
            i = number(q)
            old = [s for s in pool if not dma and s[0] == i and s[2] in seen[name]]
            if old:
                old[0][2], old[0][3] = name, old[0][3] + 1
                mark[name] = (old[0][1], old[0][3])
            else:
                pool.append([-1 if dma else i, "s%d" % len(pool), name, 16 if dma else 1])
                mark[name] = (pool[-1][1], pool[-1][3])
    for (name, q, fn, deps, dma), w in zip(ops, waits):
        for dep in w:
            q.wait_ge(T.sem[mark[dep][0]], mark[dep][1])
        if fn is not None:
            ins = fn()
            if name in needed:
                ins.then_inc(T.sem[mark[name][0]], 16 if dma else 1)
    g.wait_ge(T.sem["lall"], local["lall"])
